import numpy as np, ml_dtypes
CORES = [2,6,10,14,18,22,26,30]
N = 8
import mx_ref
BF = ml_dtypes.bfloat16
def pick(q, e):
    c = np.concatenate([q[0].reshape(128, -1, 4), np.zeros((128, 1, 4), np.uint8)], axis=1); s = np.concatenate([q[1], np.ones((16, 1), np.uint8)], axis=1)
    return (np.ascontiguousarray(c[:, e].reshape(128, -1)), np.ascontiguousarray(s[:, e]))
def join(*qs):
    return (np.concatenate([q[0] for q in qs], axis=1), np.concatenate([q[1] for q in qs], axis=1))
def put(q, e, v):
    c, s = q[0].reshape(128, -1, 4).copy(), q[1].copy(); c[:, e] = v[0].reshape(128, -1, 4); s[:, e] = v[1]
    return (c.reshape(128, -1), s)
def pk(c, s):
    return (np.ascontiguousarray(c), mx_ref.live(s))
def emit(q):
    return q[0], q[1]
def decode(q):
    o = []
    for b in range(4):
        e = np.zeros((128, 128, 4), np.float32); e[np.arange(128), np.arange(128), b] = 1
        o.append(mx_ref.matmul(mx_ref.quantize(e.reshape(128, 512).astype(BF)), q))
    return np.stack(o, axis=2).reshape(128, -1)
def f(rng, *shape):
    return mx_ref.flush((rng.standard_normal(shape, dtype=np.float32) * np.exp2(rng.integers(-2, 3, shape[:-1] + (1,)))).astype(BF))
def wide(rng, *shape, cols=0):
    v = rng.standard_normal(shape, dtype=np.float32) * np.exp2(rng.integers(-12, 13, shape)).astype(np.float32)
    if cols: v *= np.repeat(np.exp2(rng.integers(-cols, cols + 1, shape[:-2] + (1, shape[-1] // 4))) * (rng.random(shape[:-2] + (1, shape[-1] // 4)) > 0.0625), 4, axis=-1).astype(np.float32)
    return mx_ref.flush(v.astype(BF))
I, B, K, M, R = 32, 256, 8, 8, 3
H = M + M // 2
def least(v):
    v = np.array(v)
    v[np.abs(v.astype(np.float32)) < np.float32(2.0 ** -12)] = 0
    return v
def plain(rng):
    return {"it": least(f(rng, N, 128, 4 * I)), "x": least(f(rng, N, 128, 4 * B)), "w": f(rng, N, 128, 512)}
def lay(m):
    return np.ascontiguousarray(m.reshape(N, 128, 4, -1).transpose(0, 1, 3, 2)).reshape(N, 128, -1).astype(np.float32).astype(BF)
def goods(at):
    m = np.zeros((N, 512, I))
    for q in range(N):
        e = at[I * q:I * q + I]
        m[q, e, np.arange(I)] = 16
        m[q, 256 + e, np.arange(I)] = 2.0 ** -7
    return m
def wishes(at, goal, size, fine):
    m = np.zeros((N, 512, B))
    for r in range(N):
        m[r, at[goal[r]], np.arange(B)] = size[r]
        m[r, 256 + at[goal[r]], np.arange(B)] = fine[r]
    return m
def hot(rng, owners):
    return np.concatenate([I * q + rng.permutation(I)[:H] for q in owners])
def setup_inputs(rng):
    return plain(rng)
def setup_inputs_again(rng):
    at, owners = rng.permutation(256), rng.permutation(N)
    goal = I * owners[rng.integers(0, 2, (N, B))] + rng.integers(0, I, (N, B))
    size = np.full((N, B), 2.0)
    s = np.tile(1 + (np.arange(H) < H // 2), 2)
    e = hot(rng, owners[:2])
    slots = np.concatenate([[0], 1 + rng.permutation(N * K - 1)[:4 * H - 1]])
    number = np.stack([np.concatenate([[0], 1 + rng.permutation(B - 1)[:K - 1]])] + [rng.permutation(B)[:K] for r in range(1, N)])[slots // K, slots % K]
    goal[slots // K, number] = np.concatenate([e, e])
    size[slots // K, number] = 16 * np.concatenate([8 * s, 7 * s])
    return {**plain(rng), "it": lay(goods(at)), "x": lay(wishes(at, goal, size, np.zeros((N, B))))}
def setup_inputs_below(rng):
    d = plain(rng)
    low = np.argsort(rng.random((N, 128, I)), axis=1) < 64
    half = np.argsort(rng.random((N, 128, B)), axis=1) < 64
    e = rng.permutation(np.concatenate([I * q + rng.permutation(I)[:K] for q in range(N)])).reshape(N, K)
    for r in range(N):
        b = rng.permutation(B)[:K]
        half[r][:, b] = low[e[r] // I, :, e[r] % I].T
    d["it"] = ((1 + 0.25 * rng.random((N, 128, 4 * I)) + np.where(np.repeat(low, 4, axis=2), 0.0, 0.75)) * 2.0 ** 29).astype(np.float32).astype(BF)
    d["x"] = (-(1 + rng.random((N, 128, 4 * B))) * 2.0 ** 29 * np.repeat(half, 4, axis=2)).astype(np.float32)
    d["x"][d["x"] == 0] = 0
    d["x"] = d["x"].astype(BF)
    return d
def setup_inputs_near(rng):
    at, o = rng.permutation(256), int(rng.integers(0, N - 1))
    pool = I * o + np.sort(rng.permutation(I)[:2 * K])
    goal, size, fine = rng.integers(0, N * I, (N, B)), np.full((N, B), 16.0), np.zeros((N, B))
    for r in range(1, N):
        b = K + rng.permutation(B - K)[:K]
        goal[r, b] = pool[K:] if r % 2 == (N - 1) % 2 else pool[:K]
        fine[r, b] = r * 2.0 ** -7
    m = wishes(at, goal, size, fine)
    q = I * ((o + 1) % N)
    i = rng.integers(0, I - 1, B)
    j = rng.integers(i + 1, I)
    n = rng.integers(1, 8, B)
    n[:K] = 1
    n[B - K:] = 8
    m[0] = 0
    m[0, at[q + i], np.arange(B)] = 16
    m[0, at[q + j], np.arange(B)] = 16
    m[0, 256 + at[q + j], np.arange(B)] = n * 2.0 ** -7
    return {**plain(rng), "it": lay(goods(at)), "x": lay(m)}
def setup_inputs_ties(rng):
    at, owners, z = rng.permutation(256), rng.permutation(N), int(rng.integers(0, N))
    goal = rng.integers(0, N * I, (N, B))
    e = np.resize(rng.permutation(hot(rng, owners[:2])), (N - 1) * K).reshape(N - 1, K)
    goal[np.arange(N) != z, :K] = rng.permuted(e, axis=1)
    m = wishes(at, goal, np.full((N, B), 16.0), np.zeros((N, B)))
    m[z] = 0
    for q in owners[2:4]:
        e = rng.integers(0, I, B)
        e[:2] = np.min(e[:K])
        m[z, at[I * q + e], np.arange(B)] = 16
    return {**plain(rng), "it": lay(goods(at)), "x": lay(m)}
def setup_inputs_spread(rng):
    return {**plain(rng), "it": least(wide(rng, N, 128, 4 * I, cols=4)), "x": least(wide(rng, N, 128, 4 * B, cols=4))}
def check_inputs(d):
    b = []
    for k, low in (("it", 2.0 ** -12), ("x", 2.0 ** -12), ("w", 2.0 ** -30)):
        v = np.abs(d[k].astype(np.float32))
        if not (np.isfinite(v).all() and ((v == 0) | (v >= low) & (v <= 2.0 ** 30)).all()): b.append("a value of " + k)
    return b
def values(xq, g, price):
    s = np.concatenate([mx_ref.matmul(pick(xq, np.arange(128 * i, 128 * i + 128)), g) for i in range(B // 128)])
    return s + np.float32(0) - price
def reference(it, x, w):
    xq = [mx_ref.quantize(np.ascontiguousarray(x[r])) for r in range(N)]
    g = join(*[mx_ref.quantize(np.ascontiguousarray(it[q])) for q in range(N)])
    price, holder, free = np.zeros(N * I, np.float32), np.full(N * I, -1), np.ones((N, B), bool)
    ho, pr = np.zeros((N, R, I), np.float32), np.zeros((N, R, I), np.float32)
    every = np.arange(B)
    for t in range(R):
        best, who = np.zeros(N * I, np.float32), np.full(N * I, -1)
        for r in range(N):
            v = values(xq[r], g, price)
            goal = np.argmax(v, axis=1)
            large = v[every, goal]
            v[every, goal] = -np.inf
            bid = large - np.max(v, axis=1)
            c = np.flatnonzero(free[r])
            for b in c[np.argsort(-bid[c], kind="stable")[:K]]:
                i = goal[b]
                if who[i] < 0 or bid[b] > best[i]: best[i], who[i] = bid[b], B * r + b
        sold = []
        for q in range(N):
            c = np.arange(I * q, I * q + I)
            c = c[who[c] >= 0]
            sold.extend(c[np.argsort(-best[c], kind="stable")[:M]].tolist())
        n = len(sold)
        buyers = join(*[pick(xq[who[i] // B], np.array([who[i] % B])) for i in sold])
        none = np.full(N * M - n, -1)
        old = decode(pick(g, np.concatenate([np.array(sold), none])))
        new = np.float32(0.5) * (old + decode(pick(buyers, np.concatenate([np.arange(n), none]))))
        g = put(g, np.array(sold), pick(mx_ref.quantize(np.ascontiguousarray(new.astype(BF))), np.arange(n)))
        for i in sold:
            if holder[i] >= 0: free[holder[i] // B, holder[i] % B] = True
            free[who[i] // B, who[i] % B] = False
            holder[i] = who[i]
            price[i] = price[i] + best[i]
        ho[:, t], pr[:, t] = holder.reshape(N, I), price.reshape(N, I)
    y = np.stack([mx_ref.matmul(mx_ref.quantize(np.ascontiguousarray(w[r])), g) for r in range(N)])
    own = [emit(pick(g, np.arange(I * q, I * q + I))) for q in range(N)]
    return {"y": y, "oc": np.stack([a for a, b in own]), "osc": np.stack([b for a, b in own]), "ho": ho, "pr": pr}

@@ -1,0 +1,538 @@
+from concourse.bass import DstId, RemoteDMATransfer
+from concourse.mybir import dt, AluOpType as OP, AxisListType as AX, ActivationFunctionType as AF
+
+TWO_ITEMS, TWO_LIST, TWO_COLS = False, False, True
+X4, U8 = "float8_e4m3fn_x4", "uint8"
+W = 384
+SCRATCH = {
+    "F": ("sbuf", [128, 24576], "float32"), "C": ("sbuf", [128, 4096], "float32"), "CI": ("sbuf", [128, 512], "int32"),
+    "U": ("sbuf", [128, 512], "uint16"), "L": ("sbuf", [128, 192], "float32"),
+    "xb": ("sbuf", [128, 1024], "bfloat16"), "wb": ("sbuf", [128, 512], "bfloat16"), "Z": ("sbuf", [128, 520], "bfloat16"),
+    "DX": ("sbuf", [128, 1024], "float32"), "DW": ("sbuf", [128, 4 * W], "float32"), "GX": ("sbuf", [128, 96], "float32"),
+    "Xc": ("sbuf", [128, 256], X4), "Xs": ("sbuf", [128, 256], U8), "Pc": ("sbuf", [128, 256], X4), "Ps": ("sbuf", [128, 256], U8),
+    "Wc": ("sbuf", [128, 128], X4), "Ws": ("sbuf", [128, 128], U8), "Ec": ("sbuf", [128, 512], X4), "Es": ("sbuf", [128, 512], U8),
+    "Vc": ("sbuf", [128, 448], X4), "Vs": ("sbuf", [128, 448], U8), "Oc": ("sbuf", [128, 32], X4), "Os": ("sbuf", [128, 32], U8),
+    "PS": ("psum", [128, 512 * 7], "float32"),
+}
+for _s in range(4):
+    SCRATCH["T%d" % _s] = ("sbuf", [128, 512], "bfloat16")
+    SCRATCH["Sc%d" % _s] = ("sbuf", [128, 256], X4)
+    SCRATCH["Ss%d" % _s] = ("sbuf", [128, 256], U8)
+SEMAPHORES = ["qv", "qs", "qt", "qg", "sent"] + ["d%d" % i for i in range(32)] + ["a%d" % i for i in range(16)]
+
+BIG, TINY, PRED, MAG = 2.0 ** 96, 2.0 ** -90, 1.0 - 2.0 ** -24, 1.5 * 2.0 ** 23
+
+
+def A(n, a, b, s=1, p=(0, 128)):
+    return (n, a, b, s, p[0], p[1])
+
+
+def sub(v, a, b, s=1, p=None):
+    return (v[0], v[1] + a, v[1] + b, s, v[4] if p is None else p[0], v[5] if p is None else p[1])
+
+
+def rank_program(g, core, T, topo):
+    r = T.rank_of(core)
+    if r is None:
+        return
+    cores = list(T.cores)
+    ops, log = [], {}
+    Q = {"v": g.vector, "s": g.scalar, "t": g.tensor, "g": g, "y": g.sync}
+    top = {"F": 0, "C": 0, "CI": 0, "U": 0, "d": 0, "a": 0, "sent": 0}
+
+    def new(n, buf="F"):
+        a = top[buf]
+        top[buf] = a + (n + 15) // 16 * 16
+        assert top[buf] <= SCRATCH[buf][1][1]
+        return A(buf, a, a + n)
+
+    def ap(v):
+        if not isinstance(v, tuple):
+            return v
+        if v[0] == "ind":
+            return ap(v[1]).indirect(ap(v[2]))
+        return T[v[0]][v[4]:v[5], v[1]:v[2]] if v[3] == 1 else T[v[0]][v[4]:v[5], v[1]:v[2]:v[3]]
+
+    def touch(v, i, q, write, deps):
+        n, a, b, _, p0, p1 = v
+        if n == "PS":
+            a, b, p0, p1 = a // 512 * 512, (b + 511) // 512 * 512, 0, 128
+        for (a2, b2, p2, p3, j, q2, w2) in log.setdefault(n, []):
+            if j != i and a < b2 and a2 < b and p0 < p3 and p2 < p1 and (write or w2 or (n == "PS" and q2 != q)):
+                deps.add(j)
+        log[n].append((a, b, p0, p1, i, q, write))
+
+    def op(q, fn, outs, ins, tok=None):
+        i, deps = len(ops), set()
+        for v, w in [(x, False) for x in ins] + [(x, True) for x in outs]:
+            if isinstance(v, tuple):
+                if v[0] == "ind":
+                    touch(v[1], i, q, w, deps)
+                    touch(v[2], i, q, False, deps)
+                else:
+                    touch(v, i, q, w, deps)
+        ops.append({"q": q, "fn": fn, "deps": deps, "tok": tok})
+
+    def ts(o, i, s1, op0, s2=None, op1=None):
+        if op1 is None:
+            op("v", lambda: g.vector.tensor_scalar(ap(o), ap(i), ap(s1), None, op0), [o], [i, s1])
+        else:
+            op("v", lambda: g.vector.tensor_scalar(ap(o), ap(i), ap(s1), ap(s2), op0, op1), [o], [i, s1, s2])
+        return o
+
+    def tt(o, a, b, f):
+        op("v", lambda: g.vector.tensor_tensor(ap(o), ap(a), ap(b), f), [o], [a, b])
+        return o
+
+    def cp(o, i):
+        op("v", lambda: g.vector.tensor_copy(ap(o), ap(i)), [o], [i])
+        return o
+
+    def red(o, i, f=OP.add):
+        op("v", lambda: g.vector.tensor_reduce(ap(o), ap(i), AX.X, f), [o], [i])
+        return o
+
+    def scan(o, d0, d1, init, f0, f1):
+        op("v", lambda: g.vector.tensor_tensor_scan(ap(o), ap(d0), ap(d1), init, f0, f1), [o], [d0, d1])
+        return o
+
+    def tr(o, i):
+        op("v", lambda: g.vector.transpose(ap(o), ap(i)), [o], [i])
+        return o
+
+    def ms(o, c):
+        op("v", lambda: g.vector.memset(ap(o), c), [o], [])
+        return o
+
+    def act(o, i, f=AF.Identity, bias=None, scale=None, acc=None):
+        def fn():
+            k = {}
+            if bias is not None:
+                k["bias"] = ap(bias)
+            if scale is not None:
+                k["scale"] = ap(scale)
+            if acc is not None:
+                k["accum_out"] = ap(acc)
+            return g.scalar.activation(ap(o), ap(i), f, **k)
+        op("s", fn, [o, acc], [i, bias, scale])
+        return o
+
+    def quant(c, s, i):
+        op("v", lambda: g.vector.quantize_mx(ap(c), ap(s), ap(i)), [c, s], [i])
+
+    def mm(bank, lc, ls, rc, rs):
+        o = A("PS", 512 * bank, 512 * bank + rc[2] - rc[1])
+        op("t", lambda: g.tensor.matmul_mx(ap(o), ap(lc), ap(ls), ap(rc), ap(rs), True, True), [o], [lc, ls, rc, rs])
+
+    def iota(o, pat, base, cm, fl):
+        if fl:
+            op("g", lambda: g.iota(ap(o), pat, base, cm, allow_small_or_imprecise_dtypes=True), [o], [])
+        else:
+            op("g", lambda: g.iota(ap(o), pat, base, cm), [o], [])
+        return o
+
+    def raw(v):
+        if isinstance(v, tuple) and SCRATCH[v[0]][2] == X4:
+            return ap(v).bitcast(dt.uint8)
+        return ap(v)
+
+    def dma(q, o, i):
+        sem = "d%d" % top["d"]
+        top["d"] += 1
+        op(q, lambda: Q[q].dma_start(raw(o), raw(i)).then_inc(T.sem[sem], 16), [o], [i], (sem, 16))
+
+    def pick(oc, os, wc, ws, off):
+        op("v", lambda: g.vector.tensor_copy(ap(oc).bitcast(dt.uint32), ap(wc).bitcast(dt.uint32).indirect(ap(off))), [oc], [wc, off])
+        act(os, ("ind", ws, off), AF.Copy)
+
+    sib = [q for q in range(8) if q != r and topo.chip(cores[q]) == topo.chip(core)][0]
+    assert sib == r ^ 1
+    u = r % 2
+    off_chip = [q for q in range(8) if topo.chip(cores[q]) != topo.chip(core)]
+    near = lambda q: topo.mates(topo.chip(core), topo.chip(cores[q])) or topo.same_plane(topo.chip(core), topo.chip(cores[q]))
+    off_chip.sort(key=near)
+    far = [q for q in off_chip if topo.die(cores[q]) == topo.die(core)]
+    m_off = topo.mask(core, cores[off_chip[0]])
+    m_on = topo.mask(core, cores[sib]) & ~m_off
+    e_on = [e for e in topo.engines(core, cores[sib]) if m_on >> e & 1]
+    m_on2 = [sum(1 << e for e in x) for x in (e_on[:len(e_on) // 2], e_on[len(e_on) // 2:])]
+    n_off, n_on = bin(m_off).count("1"), len(e_on)
+
+    def dst(q):
+        a = topo.addr(cores[q])
+        return DstId(rid=int(a[0]), pnc=int(a[1]))
+
+    def call(parts, sem):
+        def fn():
+            return g.remote_dma_fused([RemoteDMATransfer(dst_ids=[dst(q) for q in to], dma_engine_mask=m, remote_sem=T.sem[sem],
+                                                         src=raw(s), dsts=[raw(d) for q in to]) for s, d, to, m in parts], local_sem=T.sem.sent)
+        top["sent"] += sum(bin(p[3]).count("1") for p in parts)
+        op("g", fn, [], [p[0] for p in parts], ("none", 0))
+
+    def arrive(views, count):
+        sem = "a%d" % top["a"]
+        top["a"] += 1
+        op("x", None, views, [], (sem, count))
+        return sem
+
+    def share_cols(st, n, base, two):
+        run = lambda who, k: (128 - k, 128) if who == 0 else (128, 128 + k)
+        kinds = (("Sc%d" % st, "Vc", n), ("Ss%d" % st, "Vs", 4 * n))
+        if two:
+            s1 = arrive([A(s, *run(1 - u, k)) for s, v, k in kinds], n_on)
+            call([(A(s, *run(u, k)), A(s, *run(u, k)), [sib], m) for (s, v, k), m in zip(kinds, m_on2)], s1)
+            lo, hi, src = base + n * (r - u), base + n * (r - u + 2), (128 - n, 128 + n)
+            cnt = 2 * n_off * len(far)
+        else:
+            lo, hi, src = base + n * r, base + n * (r + 1), run(u, n)
+            cnt = 2 * (n_off * len(off_chip) + n_on)
+        s2 = arrive([A(v, a, b) for s, v, k in kinds for a, b in ((base, lo), (hi, base + 8 * n)) if a < b], cnt)
+        for s, v, k in kinds:
+            parts = [(A(s, *src), A(v, lo, hi), far if two else off_chip, m_off)]
+            call(parts if two else parts + [(A(s, *src), A(v, lo, hi), [sib], m_on)], s2)
+        for s, v, k in kinds:
+            dma("y", A(v, lo, hi), A(s, *src))
+
+    def share_list(t):
+        b = 64 * t + 8 * (r - u)
+        own, oth = A("L", b + 3 + 5 * u, b + 8 + 5 * u), A("L", b + 8 - 5 * u, b + 13 - 5 * u)
+        rest = [A("L", x, y) for x, y in ((64 * t, b), (b + 16, 64 * t + 64)) if x < y]
+        if TWO_LIST:
+            call([(own, own, [sib], m_on)], arrive([oth], n_on))
+            pair = A("L", b + 3, b + 13)
+            call([(pair, pair, far, m_off)], arrive(rest, n_off * len(far)))
+        else:
+            call([(own, own, off_chip, m_off), (own, own, [sib], m_on)], arrive(rest + [oth], n_off * len(off_chip) + n_on))
+
+    def tile(st, n):
+        return (A("T%d" % st, 512 - 4 * n, 512), A("T%d" % st, 0, 512 - 4 * n)) if u == 0 else (A("T%d" % st, 0, 4 * n), A("T%d" % st, 4 * n, 512))
+
+    def quant_stage(st):
+        a = 128 * u
+        quant(A("Sc%d" % st, a, a + 128), A("Ss%d" % st, a, a + 128), A("T%d" % st, 0, 512))
+
+    dma("y", tile(0, 32)[0], T.it[:])
+    dma("y", A("xb", 0, 1024), T.x[:])
+    dma("y", A("wb", 0, 512), T.w[:])
+    PI = iota(new(1, "CI"), [[1, 1]], 0, 1, False)
+    RI = iota(new(64, "CI"), [[1, 64]], 0, 0, False)
+    IO = iota(new(516, "C"), [[1, 516]], 0, 0, True)
+    ms(tile(0, 32)[1], 0.0)
+    LM = ms(A("L", 0, 192), 0.0)
+
+    def bits(src, n, sh, mk, mul=1.0, add=0.0):
+        i = ts(new(n, "CI"), sub(src, 0, n), sh, OP.logical_shift_right, mk, OP.bitwise_and)
+        return lambda: ts(new(n, "C"), i, mul, OP.mult, add, OP.add)
+    z = [bits(PI, 1, 0, 15), bits(PI, 1, 0, 31), bits(PI, 1, 5, 3, 64.0), bits(PI, 1, 0, 127, 4.0, 3.0),
+         bits(RI, 16, 1, 3, 64.0), bits(RI, 16, 3, 1, 32.0), bits(RI, 16, 0, 1, 16.0)]
+    op("g", None, [], [LM], ("none", 0))
+    quant_stage(0)
+    share_cols(0, 32, 0, TWO_ITEMS)
+    p16, p32, a64, p43, xa, xh, xv = [f() for f in z]
+    xo = tt(new(16, "C"), xa, xh, OP.add)
+    ts(A("Z", 0, 516), IO, p43, OP.is_equal)
+    xo = tt(new(16, "C"), xo, xv, OP.add)
+    Xc, Xs = A("Xc", 0, 256), A("Xs", 0, 256)
+    quant(Xc, Xs, A("xb", 0, 1024))
+    XP = ts(new(16, "U"), xo, p16, OP.add)
+    E = [(A("Ec", 128 * b, 128 * b + 128), A("Es", 128 * b, 128 * b + 128)) for b in range(4)]
+    NEG = ms(new(256, "C"), -BIG)
+    pick(A("Pc", 0, 256), A("Ps", 0, 256), Xc, Xs, XP)
+    for b in range(4):
+        quant(E[b][0], E[b][1], A("Z", 3 - b, 515 - b))
+    for b in range(4):
+        mm(2 + b, E[b][0], E[b][1], Xc, Xs)
+    for b in range(4):
+        act(A("DX", 256 * b, 256 * b + 256), A("PS", 512 * (2 + b), 512 * (2 + b) + 256), AF.Copy, scale=0.5)
+    Wc, Ws = A("Wc", 0, 128), A("Ws", 0, 128)
+    quant(Wc, Ws, A("wb", 0, 512))
+    z = [bits(PI, 1, 5, 3, 8.0), bits(PI, 1, 0, 3, 256.0, -256.0 * r), bits(PI, 1, 0, 3, float(W)),
+         bits(PI, 1, 2, 3, 2.0, 1.0), bits(RI, 32, 1, 7), bits(RI, 32, 2, 3), bits(RI, 16, 0, 7)]
+    a8, xadd, wp, lk, mapA, mapX0, c8 = [f() for f in z]
+    CT = new(96, "C")
+    ms(sub(CT, 0, 32), PRED)
+    ms(sub(CT, 64, 96), 1.0)
+    t0 = ts(new(32, "C"), sub(IO, 0, 32), p32, OP.is_gt)
+    g0 = ts(new(1, "C"), p32, a64, OP.add, 256.0 * r, OP.add)
+    q0 = ts(new(32, "C"), sub(IO, 0, 32), a8, OP.subtract)
+    o0 = ts(new(32, "C"), sub(IO, 0, 32), -8.0 * (r % 4), OP.add)
+    TRI = ts(sub(CT, 32, 64), t0, 2.0 ** -24, OP.mult, PRED, OP.add)
+    gid = [g0, ts(new(1, "C"), g0, 32.0, OP.add)]
+    q1 = ts(new(32, "C"), q0, 8.0, OP.is_ge, -1000.0, OP.mult)
+    o1 = ts(new(32, "C"), o0, 8.0, OP.is_ge, -1000.0, OP.mult)
+    mapX1 = ts(new(32, "C"), mapX0, 4.0, OP.add)
+    LOC = new(320)
+    ts(LOC, sub(IO, 0, 320), wp, OP.add)
+    mapQ = tt(new(32, "C"), q0, q1, OP.add)
+    mapO = tt(new(32, "C"), o0, o1, OP.add)
+    ML = ts(new(16, "C"), c8, lk, OP.is_equal)
+    cst = new(8, "C")
+    for i, c in enumerate((TINY, -32767.5 / 65536, MAG, MAG / 16, -15.5 / 512)):
+        ms(sub(cst, i, i + 1), c)
+    kT, kO, kM, kM16, kC, kN, k1 = [sub(cst, i, i + 1) for i in range(7)]
+    ms(tile(1, 8)[1], 0.0)
+
+    V = [new(320), new(320)]
+    Y = new(320)
+    bank = lambda b, lo, hi: A("PS", 512 * b + lo, 512 * b + hi)
+    Vw = lambda a, b: (A("Vc", a, b), A("Vs", a, b))
+    Xp = lambda h: (A("Pc", 128 * h, 128 * h + 128), A("Ps", 128 * h, 128 * h + 128))
+    ind = lambda w, o: ("ind", w, o)
+    mine = lambda v: sub(v, 32 * r, 32 * r + 32, 1, (0, 1))
+
+    def bids(t, src, off, later_s):
+        Fs, Ss, goal, gi, key = [new(256), new(256)], [new(256), new(256)], new(2), new(2), new(2)
+        for h in range(2):
+            scan(Fs[h], src[h], NEG, -BIG, OP.max, OP.max)
+        for h in range(2):
+            scan(sub(Ss[h], 0, 255), sub(src[h], 1, 256), sub(Fs[h], 0, 255), -BIG, OP.max, OP.min)
+            act(new(256), Fs[h], AF.Sign, bias=sub(Fs[h], 255, 256), scale=-1.0, acc=sub(goal, h, h + 1))
+        for h in range(2):
+            act(sub(gi, h, h + 1), sub(goal, h, h + 1), bias=gid[h], scale=2048.0)
+            ts(sub(key, h, h + 1), sub(Fs[h], 255, 256), sub(Ss[h], 254, 255), OP.subtract, off[h], OP.add)
+        later_s()
+        k = [sub(key, 0, 1), sub(key, 1, 2)]
+        B = new(128)
+        ts(sub(B, 32, 96), sub(CT, 32, 96), k[0], OP.mult)
+        ts(sub(B, 0, 32), sub(CT, 0, 32), k[1], OP.mult)
+        ts(sub(B, 96, 128), TRI, k[1], OP.mult)
+        B = tr(new(128), B)
+        G, rk = new(128), new(2)
+        for h in range(2):
+            ts(sub(G, 64 * h, 64 * h + 64), sub(B, 64 * h, 64 * h + 64), k[h], OP.is_ge)
+        for h in range(2):
+            red(sub(rk, h, h + 1), sub(G, 64 * h, 64 * h + 64))
+        O = new(128)
+        for f, pay in enumerate((key, gi)):
+            for h in range(2):
+                ts(sub(O, 64 * f + 32 * h, 64 * f + 32 * h + 32), mapQ, sub(rk, h, h + 1), OP.is_equal, sub(pay, h, h + 1), OP.mult)
+        O = tr(new(128), O)
+        P1, P2 = new(128), new(2)
+        for f in range(2):
+            scan(sub(P1, 64 * f, 64 * f + 64, 1, (0, 64)), sub(O, 64 * f, 64 * f + 64, 1, (0, 64)), sub(O, 64 * f, 64 * f + 64, 1, (64, 128)), 0.0, OP.add, OP.add)
+        for a in (0, 32, 64, 96):
+            tt(sub(P2, 0, 2, 1, (a, a + 32)), sub(P1, 63, 128, 64, (0, 32)), sub(P1, 63, 128, 64, (32, 64)), OP.add)
+        ck, cg = sub(P2, 0, 1), sub(P2, 1, 2)
+        B = ts(new(32), TRI, ck, OP.mult)
+        y = ts(new(1), cg, -1023.5, OP.add, 2.0 ** -11, OP.mult)
+        n = act(new(1), cg, bias=kO, scale=2.0 ** -16)
+        n = act(new(1), n, bias=kM)
+        n = act(new(1), n, bias=kM16, scale=-1.0 / 16)
+        ncs = act(new(1), n, bias=kC)
+        B = tr(new(32), B)
+        gl = ts(new(1), y, MAG, OP.add, -MAG, OP.add)
+        B = ts(new(32), B, ck, OP.is_ge)
+        gs = ts(new(1), gl, 1.0 / 512, OP.mult)
+        r2 = red(new(1), B)
+        gd = ts(new(1), gl, -2048.0, OP.mult, cg, OP.add)
+        O = new(160)
+        oh = lambda o, m, pay: ts(o, m, r2, OP.is_equal, pay, OP.mult)
+        oh(sub(O, 0, 32, 2), sub(mapA, 0, 32, 2), ck)
+        oh(sub(O, 1, 32, 2), sub(mapA, 1, 32, 2), gs)
+        oh(sub(O, 32, 64), mapO, ck)
+        oh(sub(O, 64, 96), mapO, gs)
+        oh(sub(O, 128, 160), mapA, gd)
+        oh(sub(O, 96, 128), mapO, ncs)
+        O = tr(new(160), O)
+        X = new(64)
+        oh(sub(X, 0, 32), mapX0, gd)
+        m = 64 * t + 8 * (r - u) + 3 + 5 * u
+        for f in range(2):
+            act(new(32), sub(O, 96 + 32 * f, 128 + 32 * f), acc=A("L", m + 3 + f, m + 4 + f))
+        for f in range(3):
+            red(A("L", m + f, m + f + 1), sub(O, 32 * f, 32 * f + 32))
+        share_list(t)
+        oh(sub(X, 32, 64), mapX1, gd)
+        og = ts(new(1, "U"), A("L", m, m + 1), 512.0, OP.mult, 255.0, OP.min)
+        X = tr(new(64), X)
+        lr = tt(new(16), ind(LOC, og), ML, OP.mult)
+        l2, x2 = new(2), new(2)
+        for c in range(2):
+            red(sub(x2, c, c + 1), sub(X, 32 * c, 32 * c + 32))
+        for c in range(2):
+            red(sub(l2, c, c + 1), sub(lr, 8 * c, 8 * c + 8))
+        ox = ts(new(2, "U"), x2, xadd, OP.add)
+        ov = cp(new(2, "U"), l2)
+        gx = cp(A("GX", 32 * t, 32 * t + 32), ind(A("DX", 0, 1024), ox))
+        tt(tile(t + 1, 8)[0], ind(A("DW", 0, 256 + 64 * t + 3 * W), ov), gx, OP.add)
+        quant_stage(t + 1)
+        share_cols(t + 1, 8, 256 + 64 * t, TWO_COLS)
+
+    for h in range(2):
+        mm(h, *Xp(h), *Vw(0, 256))
+    for b in range(4):
+        mm(2 + b, E[b][0], E[b][1], *Vw(0, 256))
+    mm(6, Wc, Ws, *Vw(0, 256))
+    act(sub(V[1], 0, 256), bank(1, 0, 256), AF.Copy)
+
+    def first_s():
+        act(sub(V[0], 0, 256), bank(0, 0, 256), AF.Copy)
+        for b in range(4):
+            act(A("DW", W * b, W * b + 256), bank(2 + b, 0, 256), AF.Copy, scale=0.5)
+    bids(0, [bank(0, 0, 256), sub(V[1], 0, 256)], [kT, kT], first_s)
+    act(sub(Y, 0, 256), bank(6, 0, 256), AF.Copy)
+
+    z = [bits(PI, 1, 4, 1, 5.0, 3.0), bits(RI, 64, 0, 15), bits(RI, 8, 1, 3, 16.0)]
+    par, c16, gb = [f() for f in z]
+    p32b = ts(new(1, "C"), p32, 32.0, OP.add)
+    GA = ts(new(8, "U"), gb, par, OP.add)
+    GB = ts(new(8, "U"), gb, par, OP.add, 4.0, OP.add)
+    c0 = new(128, "C")
+    ts(sub(c0, 0, 64), sub(IO, 0, 64), p32, OP.is_lt)
+    ts(sub(c0, 64, 128), sub(IO, 0, 64), p32b, OP.is_lt)
+    MK = ts(new(32, "C"), sub(c16, 0, 32), p16, OP.is_equal)
+    r0 = ts(new(64, "C"), sub(IO, 0, 64), p16, OP.add, 257.0, OP.add)
+    r1 = ts(new(64, "C"), c16, 0.0, OP.is_equal)
+    ntr = [ts(new(1, "C"), x, -1.0, OP.mult, -256.0, OP.add) for x in (p32, p32b)]
+    ngid = [ts(new(1, "C"), x, -1.0, OP.mult) for x in gid]
+    CS = ts(new(128, "C"), c0, 2.0 ** -24, OP.mult, PRED, OP.add)
+    CM = ts(new(32, "C"), MK, 8.5, OP.mult, -1.0, OP.add)
+    r3 = tt(new(64, "C"), r0, r1, OP.mult)
+    ms(kN, -TINY)
+    ms(k1, 1.0)
+    TRS = ts(new(64, "C"), r3, -1.0, OP.add)
+    IW = ts(new(192, "C"), sub(IO, 256, 448), wp, OP.add)
+    H = ms(new(320), -1.0)
+    P = ms(new(320), 0.0)
+    for st in (2, 3):
+        ms(tile(st, 8)[1], 0.0)
+
+    def sales(t):
+        L = A("L", 64 * t, 64 * t + 64)
+        IN = cp(new(128), ind(L, GA))
+        t1 = tt(new(48), sub(L, 0, 48), sub(L, 16, 64), OP.add)
+        if t:
+            po = new(8, "U")
+            for x in range(2):
+                ts(sub(po, x, 8, 2), sub(L, 3 + 5 * x, 64, 16), 512.0, OP.mult, 255.0, OP.min)
+        GI = act(new(128), ind(L, GB), AF.Copy)
+        R = tr(new(128), IN)
+        ow = tt(new(37), sub(t1, 3, 40), sub(t1, 8, 45), OP.add)
+        if t:
+            PG = act(new(128), ind(P, po), AF.Copy)
+        K, G = sub(R, 0, 128, 2), sub(R, 1, 128, 2)
+        k, gs, nc = [[sub(ow, 32 * b + f, 32 * b + f + 1) for b in range(2)] for f in (1, 2, 3)]
+        half = lambda v, b: sub(v, 64 * b, 64 * b + 64)
+        Kc, e, Z, S, Bm, so = [new(128) for i in range(6)]
+        for b in range(2):
+            act(half(Z, b), G, AF.Abs, bias=nc[b])
+        for b in range(2):
+            act(half(S, b), K, AF.Sign, bias=k[b], scale=-1.0)
+            act(half(Bm, b), G, bias=gs[b], scale=-1.0)
+        for b in range(2):
+            tt(half(Kc, b), K, half(CS, b), OP.mult)
+        for b in range(2):
+            ts(half(e, b), G, gs[b], OP.is_equal)
+        gm = [ts(new(1), gs[b], 512.0, OP.mult, ntr[b], OP.add) for b in range(2)]
+        M = tt(new(128), e, Kc, OP.mult)
+        for b in range(2):
+            ts(half(so, b), half(Z, b), 1.0 / 32, OP.is_lt, k[b], OP.mult)
+        best = [red(new(1), half(M, b), OP.max) for b in range(2)]
+        lt = tt(new(128), S, Bm, OP.is_gt)
+        D = [ts(new(1), best[b], k[b], OP.is_lt, gm[b], OP.mult) for b in range(2)]
+        BT = tt(new(128), lt, so, OP.mult)
+        GI = tr(new(128), GI)
+        Wn = new(128)
+        for b in range(2):
+            ts(half(Wn, b), half(BT, b), best[b], OP.is_gt)
+        if t:
+            NP = act(new(64), tt(new(64), sub(PG, 1, 128, 2), K, OP.add), bias=kN)
+        else:
+            NP = act(new(64), K, bias=kN)
+        Wn = tr(new(128), Wn)
+        cn = [scan(new(32), sub(Wn, 32 * b, 32 * b + 32), sub(Wn, 64 + 32 * b, 96 + 32 * b), 0.0, OP.add, OP.add) for b in range(2)]
+        B = new(64)
+        for b in range(2):
+            ts(sub(B, 32 * b, 32 * b + 32), CM, sub(cn[b], 31, 32), OP.is_gt, D[b], OP.mult)
+        B = tr(new(64), B)
+        B = scan(new(64), TRS, B, 0.0, OP.max, OP.add)
+        return cp(new(4, "U"), sub(B, 15, 64, 16)), NP, sub(GI, 0, 128, 2)
+
+    for t in range(3):
+        so, NP, GI = sales(t)
+        mov = Vw(192 + 64 * t, 320 + 64 * t)
+        pos = sub(IW, 64 * t, 64 * t + 64)
+        if t < 2:
+            for h in range(2):
+                mm(h, *Xp(h), *mov)
+            for b in range(4):
+                mm(2 + b, E[b][0], E[b][1], *mov)
+            mm(6, Wc, Ws, *mov)
+            cp(ind(H, so), GI)
+            cp(ind(LOC, so), pos)
+            vn = [tt(new(64), bank(h, 64, 128), NP, OP.subtract) for h in range(2)]
+            for h in range(2):
+                cp(ind(V[h], so), vn[h])
+            nf, off = new(2), new(2)
+            for h in range(2):
+                a = act(new(256), sub(H, 0, 256), AF.Abs, bias=ngid[h])
+                act(new(256), a, AF.Relu, bias=k1, scale=-1.0, acc=sub(nf, h, h + 1))
+            act(off, nf, bias=kT, scale=-BIG)
+            dma("y", T.ho[t:t + 1, :], mine(H))
+
+            def later_s():
+                for b in range(4):
+                    act(A("DW", W * b + 256 + 64 * t, W * b + 320 + 64 * t), bank(2 + b, 64, 128), AF.Copy, scale=0.5)
+            bids(t + 1, [sub(V[0], 0, 256), sub(V[1], 0, 256)], [sub(off, 0, 1), sub(off, 1, 2)], later_s)
+            yn = act(new(64), bank(6, 64, 128), AF.Copy)
+            cp(ind(P, so), NP)
+            cp(ind(Y, so), yn)
+            dma("y", T.pr[t:t + 1, :], mine(P))
+        else:
+            mm(6, Wc, Ws, *mov)
+            cp(ind(LOC, so), pos)
+            cp(ind(H, so), GI)
+            lm = tt(new(32), sub(LOC, 32 * r, 32 * r + 32), MK, OP.mult)
+            cp(ind(P, so), NP)
+            l2 = new(2)
+            for c in range(2):
+                red(sub(l2, c, c + 1), sub(lm, 16 * c, 16 * c + 16))
+            oo = ts(new(2, "U"), l2, wp, OP.subtract)
+            dma("s", T.ho[t:t + 1, :], mine(H))
+            dma("y", T.pr[t:t + 1, :], mine(P))
+            yn = act(new(64), bank(6, 64, 128), AF.Copy)
+            pick(A("Oc", 0, 32), A("Os", 0, 32), *Vw(0, 448), oo)
+            cp(ind(Y, so), yn)
+            dma("y", T.oc[:], A("Oc", 0, 32))
+            for q in range(2):
+                dma("s", T.osc[4 * q:4 * q + 4, :], A("Os", 0, 32, 1, (32 * q, 32 * q + 4)))
+            dma("y", T.y[:], sub(Y, 0, 256))
+            for q in range(2, 4):
+                dma("sy"[q % 2], T.osc[4 * q:4 * q + 4, :], A("Os", 0, 32, 1, (32 * q, 32 * q + 4)))
+
+    used = set()
+    for o in ops:
+        last = {}
+        for j in o["deps"]:
+            if ops[j]["tok"] is None:
+                last[ops[j]["q"]] = max(last.get(ops[j]["q"], -1), j)
+        used.update(last.values())
+        o["deps"] = [j for j in o["deps"] if ops[j]["tok"] is not None] + list(last.values())
+    count, seen, total = {"v": 0, "s": 0, "t": 0, "g": 0}, {}, {"sent": top["sent"]}
+    for i, o in enumerate(ops):
+        q = o["q"]
+        if q == "x":
+            total[o["tok"][0]] = o["tok"][1]
+            continue
+        need = {}
+        for j in o["deps"]:
+            s, c = ops[j]["tok"]
+            need[s] = max(need.get(s, 0), c)
+        for s, c in sorted(need.items()):
+            if c > seen.get((q, s), 0):
+                Q[q].wait_ge(T.sem[s], c)
+                seen[(q, s)] = c
+        if o["fn"] is None:
+            continue
+        ins = o["fn"]()
+        if o["tok"] is None:
+            if i in used:
+                count[q] += 1
+                ins.then_inc(T.sem["q" + q], 1)
+                o["tok"] = ("q" + q, count[q])
+                total["q" + q] = count[q]
+        elif o["tok"][1]:
+            total[o["tok"][0]] = o["tok"][1]
+    for s, c in total.items():
+        if c > max([0] + [v for (q, s2), v in seen.items() if s2 == s]):
+            g.wait_ge(T.sem[s], c)

@@ -1,26 +1,28 @@
 from concourse.bass import DstId, RemoteDMATransfer
 from concourse.mybir import dt, AluOpType as OP, AxisListType as AX, ActivationFunctionType as AF
 
-TWO_ITEMS, TWO_LIST, TWO_COLS = False, False, True
+HELP = (3, 3, 3, 3)
 X4, U8 = "float8_e4m3fn_x4", "uint8"
 W = 384
 SCRATCH = {
-    "F": ("sbuf", [128, 24576], "float32"), "C": ("sbuf", [128, 4096], "float32"), "CI": ("sbuf", [128, 512], "int32"),
+    "F": ("sbuf", [128, 24576], "float32"), "C": ("sbuf", [128, 4096], "float32"),
     "U": ("sbuf", [128, 512], "uint16"), "L": ("sbuf", [128, 192], "float32"),
     "xb": ("sbuf", [128, 1024], "bfloat16"), "wb": ("sbuf", [128, 512], "bfloat16"), "Z": ("sbuf", [128, 520], "bfloat16"),
     "DX": ("sbuf", [128, 1024], "float32"), "DW": ("sbuf", [128, 4 * W], "float32"), "GX": ("sbuf", [128, 96], "float32"),
     "Xc": ("sbuf", [128, 256], X4), "Xs": ("sbuf", [128, 256], U8), "Pc": ("sbuf", [128, 256], X4), "Ps": ("sbuf", [128, 256], U8),
     "Wc": ("sbuf", [128, 128], X4), "Ws": ("sbuf", [128, 128], U8), "Ec": ("sbuf", [128, 512], X4), "Es": ("sbuf", [128, 512], U8),
     "Vc": ("sbuf", [128, 448], X4), "Vs": ("sbuf", [128, 448], U8), "Oc": ("sbuf", [128, 32], X4), "Os": ("sbuf", [128, 32], U8),
+    "T0": ("sbuf", [128, 512], "bfloat16"), "T1": ("sbuf", [128, 512], "bfloat16"),
     "PS": ("psum", [128, 512 * 7], "float32"),
 }
 for _s in range(4):
-    SCRATCH["T%d" % _s] = ("sbuf", [128, 512], "bfloat16")
-    SCRATCH["Sc%d" % _s] = ("sbuf", [128, 256], X4)
-    SCRATCH["Ss%d" % _s] = ("sbuf", [128, 256], U8)
-SEMAPHORES = ["qv", "qs", "qt", "qg", "sent"] + ["d%d" % i for i in range(32)] + ["a%d" % i for i in range(16)]
+    SCRATCH["Sc%d" % _s] = ("sbuf", [128, 128], X4)
+    SCRATCH["Ss%d" % _s] = ("sbuf", [128, 128], U8)
+    SCRATCH["Hs%d" % _s] = ("sbuf", [128, 32], U8)
+SEMAPHORES = ["qv", "qs", "qt", "qg", "sent"] + ["d%d" % i for i in range(32)] + ["c%d" % i for i in range(4)] + ["l%d" % i for i in range(3)]
 
 BIG, TINY, PRED, MAG = 2.0 ** 96, 2.0 ** -90, 1.0 - 2.0 ** -24, 1.5 * 2.0 ** 23
+STAGE = ((32, 0), (8, 256), (8, 320), (8, 384))
 
 
 def A(n, a, b, s=1, p=(0, 128)):
@@ -31,14 +33,49 @@ def sub(v, a, b, s=1, p=None):
     return (v[0], v[1] + a, v[1] + b, s, v[4] if p is None else p[0], v[5] if p is None else p[1])
 
 
+def wiring(topo, cores, r):
+    core = cores[r]
+    sib = [q for q in range(8) if q != r and topo.chip(cores[q]) == topo.chip(core)][0]
+    off = [q for q in range(8) if topo.chip(cores[q]) != topo.chip(core)]
+    near = lambda q: topo.mates(topo.chip(core), topo.chip(cores[q])) or topo.same_plane(topo.chip(core), topo.chip(cores[q]))
+    off.sort(key=lambda q: (topo.die(cores[q]) == topo.die(core), near(q)))
+    aide = [c for c in topo.cores_of(core) if c not in cores and topo.die(c) == topo.die(core) and all(topo.may_write(c, cores[q]) for q in off)][0]
+    m_off = topo.mask(core, cores[off[0]])
+    return sib, off, aide, m_off, topo.mask(core, cores[sib]) & ~m_off
+
+
+def place(topo, c):
+    a = topo.addr(c)
+    return DstId(rid=int(a[0]), pnc=int(a[1]))
+
+
+def aide_program(g, core, T, topo):
+    cores = list(T.cores)
+    for r in range(8):
+        sib, off, aide, m_off, m_on = wiring(topo, cores, r)
+        if aide != core:
+            continue
+        sent = 0
+        for st, (n, base) in enumerate(STAGE):
+            if HELP[st]:
+                to = off[:HELP[st]]
+                g.wait_ge(T.sem["c%d" % st], bin(m_on).count("1"))
+                g.remote_dma_fused([RemoteDMATransfer(dst_ids=[place(topo, cores[q]) for q in to], dma_engine_mask=m_off, remote_sem=T.sem["c%d" % st],
+                                                      src=T["Hs%d" % st][:, 0:n], dsts=[T.Vs[:, base + n * r:base + n * r + n] for q in to])], local_sem=T.sem.sent)
+                sent += bin(m_off).count("1")
+        if sent:
+            g.wait_ge(T.sem.sent, sent)
+
+
 def rank_program(g, core, T, topo):
     r = T.rank_of(core)
     if r is None:
+        aide_program(g, core, T, topo)
         return
     cores = list(T.cores)
     ops, log = [], {}
     Q = {"v": g.vector, "s": g.scalar, "t": g.tensor, "g": g, "y": g.sync}
-    top = {"F": 0, "C": 0, "CI": 0, "U": 0, "d": 0, "a": 0, "sent": 0}
+    top = {"F": 0, "C": 0, "U": 0, "d": 0, "sent": 0}
 
     def new(n, buf="F"):
         a = top[buf]
@@ -93,7 +130,7 @@ def rank_program(g, core, T, topo):
         return o
 
     def scan(o, d0, d1, init, f0, f1):
-        op("v", lambda: g.vector.tensor_tensor_scan(ap(o), ap(d0), ap(d1), init, f0, f1), [o], [d0, d1])
+        op("v", lambda: g.vector.tensor_tensor_scan(ap(o), ap(d0), ap(d1), ap(init), f0, f1), [o], [d0, d1, init])
         return o
 
     def tr(o, i):
@@ -117,6 +154,10 @@ def rank_program(g, core, T, topo):
         op("s", fn, [o, acc], [i, bias, scale])
         return o
 
+    def ssum(o, i):
+        act(new(i[2] - i[1]), i, acc=o)
+        return o
+
     def quant(c, s, i):
         op("v", lambda: g.vector.quantize_mx(ap(c), ap(s), ap(i)), [c, s], [i])
 
@@ -124,11 +165,13 @@ def rank_program(g, core, T, topo):
         o = A("PS", 512 * bank, 512 * bank + rc[2] - rc[1])
         op("t", lambda: g.tensor.matmul_mx(ap(o), ap(lc), ap(ls), ap(rc), ap(rs), True, True), [o], [lc, ls, rc, rs])
 
-    def iota(o, pat, base, cm, fl):
-        if fl:
-            op("g", lambda: g.iota(ap(o), pat, base, cm, allow_small_or_imprecise_dtypes=True), [o], [])
-        else:
-            op("g", lambda: g.iota(ap(o), pat, base, cm), [o], [])
+    def iota(o, pat, base=0, cm=0):
+        if o is None:
+            n = 1
+            for s, c in pat:
+                n *= c
+            o = new(n, "C")
+        op("g", lambda: g.iota(ap(o), pat, base, cm, allow_small_or_imprecise_dtypes=True), [o], [])
         return o
 
     def raw(v):
@@ -145,167 +188,147 @@ def rank_program(g, core, T, topo):
         op("v", lambda: g.vector.tensor_copy(ap(oc).bitcast(dt.uint32), ap(wc).bitcast(dt.uint32).indirect(ap(off))), [oc], [wc, off])
         act(os, ("ind", ws, off), AF.Copy)
 
-    sib = [q for q in range(8) if q != r and topo.chip(cores[q]) == topo.chip(core)][0]
+    sib, off_chip, aide, m_off, m_on = wiring(topo, cores, r)
     assert sib == r ^ 1
     u = r % 2
-    off_chip = [q for q in range(8) if topo.chip(cores[q]) != topo.chip(core)]
-    near = lambda q: topo.mates(topo.chip(core), topo.chip(cores[q])) or topo.same_plane(topo.chip(core), topo.chip(cores[q]))
-    off_chip.sort(key=near)
-    far = [q for q in off_chip if topo.die(cores[q]) == topo.die(core)]
-    m_off = topo.mask(core, cores[off_chip[0]])
-    m_on = topo.mask(core, cores[sib]) & ~m_off
-    e_on = [e for e in topo.engines(core, cores[sib]) if m_on >> e & 1]
-    m_on2 = [sum(1 << e for e in x) for x in (e_on[:len(e_on) // 2], e_on[len(e_on) // 2:])]
-    n_off, n_on = bin(m_off).count("1"), len(e_on)
-
-    def dst(q):
-        a = topo.addr(cores[q])
-        return DstId(rid=int(a[0]), pnc=int(a[1]))
+    n_off, n_on = bin(m_off).count("1"), bin(m_on).count("1")
 
     def call(parts, sem):
         def fn():
-            return g.remote_dma_fused([RemoteDMATransfer(dst_ids=[dst(q) for q in to], dma_engine_mask=m, remote_sem=T.sem[sem],
-                                                         src=raw(s), dsts=[raw(d) for q in to]) for s, d, to, m in parts], local_sem=T.sem.sent)
-        top["sent"] += sum(bin(p[3]).count("1") for p in parts)
+            return g.remote_dma_fused([RemoteDMATransfer(dst_ids=[place(topo, c) for c, d in to], dma_engine_mask=m, remote_sem=T.sem[sem],
+                                                         src=raw(s), dsts=[raw(d) for c, d in to]) for s, to, m in parts], local_sem=T.sem.sent)
+        top["sent"] += sum(bin(p[2]).count("1") for p in parts)
         op("g", fn, [], [p[0] for p in parts], ("none", 0))
 
-    def arrive(views, count):
-        sem = "a%d" % top["a"]
-        top["a"] += 1
+    def arrive(views, sem, count):
         op("x", None, views, [], (sem, count))
         return sem
 
-    def share_cols(st, n, base, two):
-        run = lambda who, k: (128 - k, 128) if who == 0 else (128, 128 + k)
-        kinds = (("Sc%d" % st, "Vc", n), ("Ss%d" % st, "Vs", 4 * n))
-        if two:
-            s1 = arrive([A(s, *run(1 - u, k)) for s, v, k in kinds], n_on)
-            call([(A(s, *run(u, k)), A(s, *run(u, k)), [sib], m) for (s, v, k), m in zip(kinds, m_on2)], s1)
-            lo, hi, src = base + n * (r - u), base + n * (r - u + 2), (128 - n, 128 + n)
-            cnt = 2 * n_off * len(far)
-        else:
-            lo, hi, src = base + n * r, base + n * (r + 1), run(u, n)
-            cnt = 2 * (n_off * len(off_chip) + n_on)
-        s2 = arrive([A(v, a, b) for s, v, k in kinds for a, b in ((base, lo), (hi, base + 8 * n)) if a < b], cnt)
-        for s, v, k in kinds:
-            parts = [(A(s, *src), A(v, lo, hi), far if two else off_chip, m_off)]
-            call(parts if two else parts + [(A(s, *src), A(v, lo, hi), [sib], m_on)], s2)
-        for s, v, k in kinds:
-            dma("y", A(v, lo, hi), A(s, *src))
+    def share_cols(st):
+        n, base = STAGE[st]
+        lo, hi, a = base + n * r, base + n * (r + 1), max(st - 1, 0) * n
+        sc, ss, vc, vs = A("Sc%d" % st, a, a + n), A("Ss%d" % st, a, a + n), A("Vc", lo, hi), A("Vs", lo, hi)
+        sem = arrive([A(v, x, y) for v in ("Vc", "Vs") for x, y in ((base, lo), (hi, base + 8 * n)) if x < y], "c%d" % st, 2 * (n_off * len(off_chip) + n_on))
+        to = lambda qs, d: [(cores[q], d) for q in qs]
+        call([(ss, [(aide, A("Hs%d" % st, 0, n))] + to([sib], vs), m_on), (ss, to(off_chip[HELP[st]:], vs), m_off)], sem)
+        call([(sc, to(off_chip, vc), m_off), (sc, to([sib], vc), m_on)], sem)
+        dma("y", vc, sc)
+        dma("y", vs, ss)
 
     def share_list(t):
         b = 64 * t + 8 * (r - u)
         own, oth = A("L", b + 3 + 5 * u, b + 8 + 5 * u), A("L", b + 8 - 5 * u, b + 13 - 5 * u)
         rest = [A("L", x, y) for x, y in ((64 * t, b), (b + 16, 64 * t + 64)) if x < y]
-        if TWO_LIST:
-            call([(own, own, [sib], m_on)], arrive([oth], n_on))
-            pair = A("L", b + 3, b + 13)
-            call([(pair, pair, far, m_off)], arrive(rest, n_off * len(far)))
-        else:
-            call([(own, own, off_chip, m_off), (own, own, [sib], m_on)], arrive(rest + [oth], n_off * len(off_chip) + n_on))
-
-    def tile(st, n):
-        return (A("T%d" % st, 512 - 4 * n, 512), A("T%d" % st, 0, 512 - 4 * n)) if u == 0 else (A("T%d" % st, 0, 4 * n), A("T%d" % st, 4 * n, 512))
+        call([(own, [(cores[q], own) for q in off_chip], m_off), (own, [(cores[sib], own)], m_on)],
+             arrive(rest + [oth], "l%d" % t, n_off * len(off_chip) + n_on))
 
     def quant_stage(st):
-        a = 128 * u
-        quant(A("Sc%d" % st, a, a + 128), A("Ss%d" % st, a, a + 128), A("T%d" % st, 0, 512))
+        quant(A("Sc%d" % st, 0, 128), A("Ss%d" % st, 0, 128), A("T%d" % min(st, 1), 0, 512))
 
-    dma("y", tile(0, 32)[0], T.it[:])
+    dma("y", A("T0", 0, 128), T.it[:])
     dma("y", A("xb", 0, 1024), T.x[:])
     dma("y", A("wb", 0, 512), T.w[:])
-    PI = iota(new(1, "CI"), [[1, 1]], 0, 1, False)
-    RI = iota(new(64, "CI"), [[1, 64]], 0, 0, False)
-    IO = iota(new(516, "C"), [[1, 516]], 0, 0, True)
-    ms(tile(0, 32)[1], 0.0)
+    RW = new(256, "C")
+    for i, (pat, base) in enumerate((([[1, 32]], 0), ([[0, 2], [1, 16]], 0), ([[0, 8], [256, 4]], -256 * r), ([[0, 8], [W, 4]], 0),
+                                     ([[0, 2], [2, 4], [0, 4]], 1), ([[5, 2], [0, 16]], 3), ([[0, 4], [1, 8]], 0), ([[0, 4], [16, 4], [5, 2]], 7))):
+        iota(sub(RW, 32 * i, 32 * i + 32), pat, base)
+    ms(A("T0", 128, 512), 0.0)
     LM = ms(A("L", 0, 192), 0.0)
-
-    def bits(src, n, sh, mk, mul=1.0, add=0.0):
-        i = ts(new(n, "CI"), sub(src, 0, n), sh, OP.logical_shift_right, mk, OP.bitwise_and)
-        return lambda: ts(new(n, "C"), i, mul, OP.mult, add, OP.add)
-    z = [bits(PI, 1, 0, 15), bits(PI, 1, 0, 31), bits(PI, 1, 5, 3, 64.0), bits(PI, 1, 0, 127, 4.0, 3.0),
-         bits(RI, 16, 1, 3, 64.0), bits(RI, 16, 3, 1, 32.0), bits(RI, 16, 0, 1, 16.0)]
+    cst = new(16, "C")
+    for i, c in enumerate((TINY, -32767.5 / 65536, MAG, -MAG * 32768, -TINY, 1.0, 256.0, -1.0, PRED, -256.0, -0.25, 0.25)):
+        ms(sub(cst, i, i + 1), c)
+    kT, kO, kM, kM15, kN, k1, k256, km1, kP, km256, kmq, kq = [sub(cst, i, i + 1) for i in range(12)]
     op("g", None, [], [LM], ("none", 0))
     quant_stage(0)
-    share_cols(0, 32, 0, TWO_ITEMS)
-    p16, p32, a64, p43, xa, xh, xv = [f() for f in z]
-    xo = tt(new(16, "C"), xa, xh, OP.add)
-    ts(A("Z", 0, 516), IO, p43, OP.is_equal)
-    xo = tt(new(16, "C"), xo, xv, OP.add)
+    share_cols(0)
+    IO = iota(None, [[1, 516]])
+    p43, xo, p2 = iota(None, [[1, 1]], 3, 4), iota(None, [[32, 2], [64, 4], [16, 2]]), iota(None, [[32, 2]], 256 * r, 2)
+    MP = new(224, "C")
+    for i, (pat, base) in enumerate((([[1000, 4], [1, 8]], -1000 * (r % 4)), ([[0, 2], [1, 8], [1000, 2]], 0), ([[0, 2], [1, 4], [0, 4]], 0),
+                                     ([[0, 2], [1, 4], [0, 4]], 4), ([[0, 2], [1, 8], [-1000, 2]], 1000))):
+        iota(sub(MP, 32 * i, 32 * i + 32), pat, base)
+    mq, gb, trs = iota(None, [[1024, 4], [1, 8]], 0, -32), iota(None, [[16, 4], [0, 2]]), iota(None, [[16, 4], [-1000, 16]], 256)
+    P = ms(new(320), 0.0)
     Xc, Xs = A("Xc", 0, 256), A("Xs", 0, 256)
     quant(Xc, Xs, A("xb", 0, 1024))
+    RT = tr(new(256, "C"), RW)
+    p32, p16, xadd, wp, lk, par, p8, gw = [sub(RT, 32 * i, 32 * i + 1) for i in range(8)]
+    Wc, Ws = A("Wc", 0, 128), A("Ws", 0, 128)
+    quant(Wc, Ws, A("wb", 0, 512))
+    CT = new(96, "C")
+    ms(sub(CT, 0, 32), PRED)
+    ms(sub(CT, 64, 96), 1.0)
+    ms(A("T1", 0, 512), 0.0)
+    ts(A("Z", 0, 516), IO, p43, OP.is_equal)
     XP = ts(new(16, "U"), xo, p16, OP.add)
     E = [(A("Ec", 128 * b, 128 * b + 128), A("Es", 128 * b, 128 * b + 128)) for b in range(4)]
-    NEG = ms(new(256, "C"), -BIG)
-    pick(A("Pc", 0, 256), A("Ps", 0, 256), Xc, Xs, XP)
     for b in range(4):
         quant(E[b][0], E[b][1], A("Z", 3 - b, 515 - b))
+    pick(A("Pc", 0, 256), A("Ps", 0, 256), Xc, Xs, XP)
     for b in range(4):
         mm(2 + b, E[b][0], E[b][1], Xc, Xs)
     for b in range(4):
         act(A("DX", 256 * b, 256 * b + 256), A("PS", 512 * (2 + b), 512 * (2 + b) + 256), AF.Copy, scale=0.5)
-    Wc, Ws = A("Wc", 0, 128), A("Ws", 0, 128)
-    quant(Wc, Ws, A("wb", 0, 512))
-    z = [bits(PI, 1, 5, 3, 8.0), bits(PI, 1, 0, 3, 256.0, -256.0 * r), bits(PI, 1, 0, 3, float(W)),
-         bits(PI, 1, 2, 3, 2.0, 1.0), bits(RI, 32, 1, 7), bits(RI, 32, 2, 3), bits(RI, 16, 0, 7)]
-    a8, xadd, wp, lk, mapA, mapX0, c8 = [f() for f in z]
-    CT = new(96, "C")
-    ms(sub(CT, 0, 32), PRED)
-    ms(sub(CT, 64, 96), 1.0)
-    t0 = ts(new(32, "C"), sub(IO, 0, 32), p32, OP.is_gt)
-    g0 = ts(new(1, "C"), p32, a64, OP.add, 256.0 * r, OP.add)
-    q0 = ts(new(32, "C"), sub(IO, 0, 32), a8, OP.subtract)
-    o0 = ts(new(32, "C"), sub(IO, 0, 32), -8.0 * (r % 4), OP.add)
-    TRI = ts(sub(CT, 32, 64), t0, 2.0 ** -24, OP.mult, PRED, OP.add)
-    gid = [g0, ts(new(1, "C"), g0, 32.0, OP.add)]
-    q1 = ts(new(32, "C"), q0, 8.0, OP.is_ge, -1000.0, OP.mult)
-    o1 = ts(new(32, "C"), o0, 8.0, OP.is_ge, -1000.0, OP.mult)
-    mapX1 = ts(new(32, "C"), mapX0, 4.0, OP.add)
-    LOC = new(320)
-    ts(LOC, sub(IO, 0, 320), wp, OP.add)
-    mapQ = tt(new(32, "C"), q0, q1, OP.add)
-    mapO = tt(new(32, "C"), o0, o1, OP.add)
-    ML = ts(new(16, "C"), c8, lk, OP.is_equal)
-    cst = new(8, "C")
-    for i, c in enumerate((TINY, -32767.5 / 65536, MAG, MAG / 16, -15.5 / 512)):
-        ms(sub(cst, i, i + 1), c)
-    kT, kO, kM, kM16, kC, kN, k1 = [sub(cst, i, i + 1) for i in range(7)]
-    ms(tile(1, 8)[1], 0.0)
+    t0 = ts(new(32, "C"), sub(IO, 0, 32), p32, OP.is_gt, 2.0 ** -24, OP.mult)
+    ML = ts(new(16, "C"), sub(RW, 192, 208), lk, OP.is_equal)
+    CM = ts(new(32, "C"), sub(RW, 32, 64), p16, OP.is_equal, 8.0, OP.mult)
+    TRI = ts(sub(CT, 32, 64), t0, PRED, OP.add)
+    sl = tr(new(32, "C"), sub(MP, 128, 160))
+    GA = ts(new(8, "U"), gb, par, OP.add)
+    GB = ts(new(8, "U"), gb, par, OP.add, 4.0, OP.add)
+    GW = cp(new(1, "U"), gw)
+    slot = ts(new(1, "C"), sub(sl, 0, 1), 8.0, OP.is_lt, sub(sl, 0, 1), OP.mult)
+    gid2 = ts(new(2, "C"), p2, p32, OP.subtract)
+    gid = [sub(gid2, h, h + 1) for h in range(2)]
+    q32 = ts(new(1, "C"), p32, 32.0, OP.mult)
+    cp(sub(MP, 160, 192), sub(MP, 0, 32))
+    cp(sub(MP, 192, 224), sub(MP, 128, 160))
+    mapQ = ts(new(32, "C"), mq, q32, OP.add)
+    ngid2 = ts(new(2, "C"), gid2, -1.0, OP.mult)
+    ngid = [sub(ngid2, h, h + 1) for h in range(2)]
+    ntr = [ts(new(1, "C"), p32, -1.0, OP.mult, -256.0 - 32 * b, OP.add) for b in range(2)]
+    kb1, kb2 = ts(new(1, "C"), p8, -32.0, OP.add, 1.0 / 128, OP.mult), ts(new(1, "C"), p8, 4096.0, OP.add, 1.0 / 16384, OP.mult)
+    TRS = ts(new(64, "C"), trs, p16, OP.add)
+    LOC = act(new(320), sub(IO, 0, 320), bias=wp)
+    IW = act(new(192, "C"), sub(IO, 256, 448), bias=wp)
+    H = act(new(320), P, bias=km1)
 
     V = [new(320), new(320)]
     Y = new(320)
+    OG = new(4, "U")
     bank = lambda b, lo, hi: A("PS", 512 * b + lo, 512 * b + hi)
     Vw = lambda a, b: (A("Vc", a, b), A("Vs", a, b))
     Xp = lambda h: (A("Pc", 128 * h, 128 * h + 128), A("Ps", 128 * h, 128 * h + 128))
     ind = lambda w, o: ("ind", w, o)
     mine = lambda v: sub(v, 32 * r, 32 * r + 32, 1, (0, 1))
 
-    def bids(t, src, off, later_s):
+    def bids(t, src, off, later_s, after_list):
         Fs, Ss, goal, gi, key = [new(256), new(256)], [new(256), new(256)], new(2), new(2), new(2)
-        for h in range(2):
-            scan(Fs[h], src[h], NEG, -BIG, OP.max, OP.max)
-        for h in range(2):
-            scan(sub(Ss[h], 0, 255), sub(src[h], 1, 256), sub(Fs[h], 0, 255), -BIG, OP.max, OP.min)
-            act(new(256), Fs[h], AF.Sign, bias=sub(Fs[h], 255, 256), scale=-1.0, acc=sub(goal, h, h + 1))
-        for h in range(2):
-            act(sub(gi, h, h + 1), sub(goal, h, h + 1), bias=gid[h], scale=2048.0)
-            ts(sub(key, h, h + 1), sub(Fs[h], 255, 256), sub(Ss[h], 254, 255), OP.subtract, off[h], OP.add)
-        later_s()
         k = [sub(key, 0, 1), sub(key, 1, 2)]
         B = new(128)
-        ts(sub(B, 32, 96), sub(CT, 32, 96), k[0], OP.mult)
+        for h in range(2):
+            scan(Fs[h], src[h], src[h] if t else sub(P, 0, 256), -BIG, OP.max, OP.max if t else OP.add)
+            act(new(256), Fs[h], AF.Sign, bias=sub(Fs[h], 255, 256), scale=-1.0, acc=sub(goal, h, h + 1))
+            scan(sub(Ss[h], 0, 255), sub(src[h], 1, 256), sub(Fs[h], 0, 255), -BIG, OP.max, OP.min)
+            if h == 0:
+                act(k[0], act(new(1), sub(Ss[0], 254, 255), bias=sub(Fs[0], 255, 256), scale=-1.0), bias=off[0])
+                act(sub(B, 32, 96), sub(CT, 32, 96), scale=k[0])
+        ts(k[1], sub(Fs[1], 255, 256), sub(Ss[1], 254, 255), OP.subtract, off[1], OP.add)
+        for h in range(2):
+            act(sub(gi, h, h + 1), sub(goal, h, h + 1), bias=gid[h], scale=2048.0)
+        later_s()
         ts(sub(B, 0, 32), sub(CT, 0, 32), k[1], OP.mult)
         ts(sub(B, 96, 128), TRI, k[1], OP.mult)
         B = tr(new(128), B)
-        G, rk = new(128), new(2)
-        for h in range(2):
+        G, rk = new(128), [new(1), new(1)]
+        for h in (1, 0):
             ts(sub(G, 64 * h, 64 * h + 64), sub(B, 64 * h, 64 * h + 64), k[h], OP.is_ge)
-        for h in range(2):
-            red(sub(rk, h, h + 1), sub(G, 64 * h, 64 * h + 64))
+        (ssum if t else red)(rk[1], sub(G, 64, 128))
+        red(rk[0], sub(G, 0, 64))
         O = new(128)
-        for f, pay in enumerate((key, gi)):
-            for h in range(2):
-                ts(sub(O, 64 * f + 32 * h, 64 * f + 32 * h + 32), mapQ, sub(rk, h, h + 1), OP.is_equal, sub(pay, h, h + 1), OP.mult)
+        for h in range(2):
+            for f, pay in enumerate((key, gi)):
+                ts(sub(O, 64 * f + 32 * h, 64 * f + 32 * h + 32), mapQ, rk[h], OP.is_equal, sub(pay, h, h + 1), OP.mult)
         O = tr(new(128), O)
         P1, P2 = new(128), new(2)
         for f in range(2):
@@ -317,46 +340,48 @@ def rank_program(g, core, T, topo):
         y = ts(new(1), cg, -1023.5, OP.add, 2.0 ** -11, OP.mult)
         n = act(new(1), cg, bias=kO, scale=2.0 ** -16)
         n = act(new(1), n, bias=kM)
-        n = act(new(1), n, bias=kM16, scale=-1.0 / 16)
-        ncs = act(new(1), n, bias=kC)
+        n = act(new(1), n, bias=kM15, scale=32768.0)
         B = tr(new(32), B)
         gl = ts(new(1), y, MAG, OP.add, -MAG, OP.add)
         B = ts(new(32), B, ck, OP.is_ge)
-        gs = ts(new(1), gl, 1.0 / 512, OP.mult)
+        gs = ts(new(1), gl, 256.0, OP.mult, 8.0 * r, OP.add)
         r2 = red(new(1), B)
+        cc = act(new(1), gs, bias=n)
         gd = ts(new(1), gl, -2048.0, OP.mult, cg, OP.add)
-        O = new(160)
-        oh = lambda o, m, pay: ts(o, m, r2, OP.is_equal, pay, OP.mult)
-        oh(sub(O, 0, 32, 2), sub(mapA, 0, 32, 2), ck)
-        oh(sub(O, 1, 32, 2), sub(mapA, 1, 32, 2), gs)
-        oh(sub(O, 32, 64), mapO, ck)
-        oh(sub(O, 64, 96), mapO, gs)
-        oh(sub(O, 128, 160), mapA, gd)
-        oh(sub(O, 96, 128), mapO, ncs)
-        O = tr(new(160), O)
-        X = new(64)
-        oh(sub(X, 0, 32), mapX0, gd)
+        O = new(288)
+        oh = lambda a, b, m, pay: ts(sub(O, a, b), sub(MP, m, m + b - a), r2, OP.is_equal, pay, OP.mult)
+        oh(0, 64, 0, ck)
+        oh(128, 192, 160, gl)
+        oh(64, 128, 128, cc)
+        oh(192, 288, 32, gd)
+        Ot = new(288)
+        tr(sub(Ot, 0, 224), sub(O, 0, 224))
         m = 64 * t + 8 * (r - u) + 3 + 5 * u
-        for f in range(2):
-            act(new(32), sub(O, 96 + 32 * f, 128 + 32 * f), acc=A("L", m + 3 + f, m + 4 + f))
-        for f in range(3):
-            red(A("L", m + f, m + f + 1), sub(O, 32 * f, 32 * f + 32))
+        col = lambda f: A("L", m + f, m + f + 1)
+        blk = lambda a, b: sub(Ot, 32 * a, 32 * b)
+        ssum(col(1), blk(0, 1))
+        red(col(0), blk(1, 3))
+        red(col(4), blk(5, 7))
+        ssum(col(3), blk(4, 5))
+        red(col(2), blk(3, 4))
         share_list(t)
-        oh(sub(X, 32, 64), mapX1, gd)
-        og = ts(new(1, "U"), A("L", m, m + 1), 512.0, OP.mult, 255.0, OP.min)
-        X = tr(new(64), X)
-        lr = tt(new(16), ind(LOC, og), ML, OP.mult)
+        og = ts(sub(OG, 2, 3) if t == 0 else sub(OG, 0, 1) if t == 1 else new(1, "U"), col(4), 255.0, OP.min)
+        tr(sub(Ot, 224, 288), sub(O, 224, 288))
+        after_list()
         l2, x2 = new(2), new(2)
         for c in range(2):
-            red(sub(x2, c, c + 1), sub(X, 32 * c, 32 * c + 32))
+            ssum(sub(x2, c, c + 1), blk(7 + c, 8 + c))
+        lr = tt(new(16), ind(LOC, og), ML, OP.mult)
+        ox = ts(new(2, "U"), x2, xadd, OP.add)
         for c in range(2):
             red(sub(l2, c, c + 1), sub(lr, 8 * c, 8 * c + 8))
-        ox = ts(new(2, "U"), x2, xadd, OP.add)
+        gx = act(A("GX", 32 * t, 32 * t + 32), ind(A("DX", 0, 1024), ox), AF.Copy)
         ov = cp(new(2, "U"), l2)
-        gx = cp(A("GX", 32 * t, 32 * t + 32), ind(A("DX", 0, 1024), ox))
-        tt(tile(t + 1, 8)[0], ind(A("DW", 0, 256 + 64 * t + 3 * W), ov), gx, OP.add)
+        tt(A("T1", 32 * t, 32 * t + 32), ind(A("DW", 0, 256 + 64 * t + 3 * W), ov), gx, OP.add)
         quant_stage(t + 1)
-        share_cols(t + 1, 8, 256 + 64 * t, TWO_COLS)
+        share_cols(t + 1)
+        if t == 0:
+            cp(sub(OG, 1, 2), og)
 
     for h in range(2):
         mm(h, *Xp(h), *Vw(0, 256))
@@ -366,86 +391,54 @@ def rank_program(g, core, T, topo):
     act(sub(V[1], 0, 256), bank(1, 0, 256), AF.Copy)
 
     def first_s():
-        act(sub(V[0], 0, 256), bank(0, 0, 256), AF.Copy)
         for b in range(4):
             act(A("DW", W * b, W * b + 256), bank(2 + b, 0, 256), AF.Copy, scale=0.5)
-    bids(0, [bank(0, 0, 256), sub(V[1], 0, 256)], [kT, kT], first_s)
+    bids(0, [bank(0, 0, 256), sub(V[1], 0, 256)], [kT, kT], first_s, lambda: None)
+    act(sub(V[0], 0, 256), bank(0, 0, 256), AF.Copy)
     act(sub(Y, 0, 256), bank(6, 0, 256), AF.Copy)
-
-    z = [bits(PI, 1, 4, 1, 5.0, 3.0), bits(RI, 64, 0, 15), bits(RI, 8, 1, 3, 16.0)]
-    par, c16, gb = [f() for f in z]
-    p32b = ts(new(1, "C"), p32, 32.0, OP.add)
-    GA = ts(new(8, "U"), gb, par, OP.add)
-    GB = ts(new(8, "U"), gb, par, OP.add, 4.0, OP.add)
-    c0 = new(128, "C")
-    ts(sub(c0, 0, 64), sub(IO, 0, 64), p32, OP.is_lt)
-    ts(sub(c0, 64, 128), sub(IO, 0, 64), p32b, OP.is_lt)
-    MK = ts(new(32, "C"), sub(c16, 0, 32), p16, OP.is_equal)
-    r0 = ts(new(64, "C"), sub(IO, 0, 64), p16, OP.add, 257.0, OP.add)
-    r1 = ts(new(64, "C"), c16, 0.0, OP.is_equal)
-    ntr = [ts(new(1, "C"), x, -1.0, OP.mult, -256.0, OP.add) for x in (p32, p32b)]
-    ngid = [ts(new(1, "C"), x, -1.0, OP.mult) for x in gid]
-    CS = ts(new(128, "C"), c0, 2.0 ** -24, OP.mult, PRED, OP.add)
-    CM = ts(new(32, "C"), MK, 8.5, OP.mult, -1.0, OP.add)
-    r3 = tt(new(64, "C"), r0, r1, OP.mult)
-    ms(kN, -TINY)
-    ms(k1, 1.0)
-    TRS = ts(new(64, "C"), r3, -1.0, OP.add)
-    IW = ts(new(192, "C"), sub(IO, 256, 448), wp, OP.add)
-    H = ms(new(320), -1.0)
-    P = ms(new(320), 0.0)
-    for st in (2, 3):
-        ms(tile(st, 8)[1], 0.0)
 
     def sales(t):
         L = A("L", 64 * t, 64 * t + 64)
-        IN = cp(new(128), ind(L, GA))
         t1 = tt(new(48), sub(L, 0, 48), sub(L, 16, 64), OP.add)
-        if t:
-            po = new(8, "U")
-            for x in range(2):
-                ts(sub(po, x, 8, 2), sub(L, 3 + 5 * x, 64, 16), 512.0, OP.mult, 255.0, OP.min)
         GI = act(new(128), ind(L, GB), AF.Copy)
-        R = tr(new(128), IN)
+        IN = ts(new(128), ind(L, GA), slot, OP.add)
         ow = tt(new(37), sub(t1, 3, 40), sub(t1, 8, 45), OP.add)
-        if t:
-            PG = act(new(128), ind(P, po), AF.Copy)
+        R = tr(new(128), IN)
         K, G = sub(R, 0, 128, 2), sub(R, 1, 128, 2)
-        k, gs, nc = [[sub(ow, 32 * b + f, 32 * b + f + 1) for b in range(2)] for f in (1, 2, 3)]
+        k, gl = [[sub(ow, 32 * b + f, 32 * b + f + 1) for b in range(2)] for f in (1, 3)]
+        b1 = act(new(2), sub(ow, 2, 35, 32), bias=kb1, scale=1.0 / 128)
+        b2 = act(new(2), sub(ow, 2, 35, 32), bias=kb2, scale=1.0 / 16384)
         half = lambda v, b: sub(v, 64 * b, 64 * b + 64)
-        Kc, e, Z, S, Bm, so = [new(128) for i in range(6)]
-        for b in range(2):
-            act(half(Z, b), G, AF.Abs, bias=nc[b])
+        S, Q1, Q2, X1, X2, Wn = [new(128) for i in range(6)]
         for b in range(2):
             act(half(S, b), K, AF.Sign, bias=k[b], scale=-1.0)
-            act(half(Bm, b), G, bias=gs[b], scale=-1.0)
+            act(half(Q1, b), G, AF.Square, bias=sub(b1, b, b + 1), scale=-1.0 / 128)
         for b in range(2):
-            tt(half(Kc, b), K, half(CS, b), OP.mult)
-        for b in range(2):
-            ts(half(e, b), G, gs[b], OP.is_equal)
-        gm = [ts(new(1), gs[b], 512.0, OP.mult, ntr[b], OP.add) for b in range(2)]
-        M = tt(new(128), e, Kc, OP.mult)
-        for b in range(2):
-            ts(half(so, b), half(Z, b), 1.0 / 32, OP.is_lt, k[b], OP.mult)
-        best = [red(new(1), half(M, b), OP.max) for b in range(2)]
-        lt = tt(new(128), S, Bm, OP.is_gt)
-        D = [ts(new(1), best[b], k[b], OP.is_lt, gm[b], OP.mult) for b in range(2)]
-        BT = tt(new(128), lt, so, OP.mult)
+            act(half(Q2, b), G, AF.Square, bias=sub(b2, b, b + 1), scale=-1.0 / 16384)
         GI = tr(new(128), GI)
-        Wn = new(128)
-        for b in range(2):
-            ts(half(Wn, b), half(BT, b), best[b], OP.is_gt)
         if t:
-            NP = act(new(64), tt(new(64), sub(PG, 1, 128, 2), K, OP.add), bias=kN)
-        else:
-            NP = act(new(64), K, bias=kN)
+            po = ts(new(16, "U"), ind(L, GW), 255.0, OP.min)
+        for b in range(2):
+            tt(half(X1, b), half(S, b), half(Q1, b), OP.add)
+        best = [red(new(1), half(X1, b), OP.min) for b in range(2)]
+        gm = [act(new(1), gl[b], bias=ntr[b]) for b in range(2)]
+        lose = [act(new(1), best[b], bias=k256, scale=-4096.0) for b in range(2)]
+        NP = act(new(64), K, bias=kN)
+        if t:
+            PG = act(new(128), ind(P, sub(po, 0, 8)), AF.Copy)
+        for b in range(2):
+            tt(half(X2, b), half(Q2, b), half(S, b), OP.subtract)
+        for b in range(2):
+            ts(half(Wn, b), half(X2, b), 0.06, OP.max, best[b], OP.is_lt)
         Wn = tr(new(128), Wn)
-        cn = [scan(new(32), sub(Wn, 32 * b, 32 * b + 32), sub(Wn, 64 + 32 * b, 96 + 32 * b), 0.0, OP.add, OP.add) for b in range(2)]
+        cn = [scan(new(32), sub(Wn, 32 * b, 32 * b + 32), sub(Wn, 64 + 32 * b, 96 + 32 * b), lose[b], OP.add, OP.add) for b in range(2)]
         B = new(64)
         for b in range(2):
-            ts(sub(B, 32 * b, 32 * b + 32), CM, sub(cn[b], 31, 32), OP.is_gt, D[b], OP.mult)
+            ts(sub(B, 32 * b, 32 * b + 32), CM, sub(cn[b], 31, 32), OP.is_gt, gm[b], OP.mult)
         B = tr(new(64), B)
         B = scan(new(64), TRS, B, 0.0, OP.max, OP.add)
+        if t:
+            NP = tt(new(64), sub(PG, 1, 128, 2), NP, OP.add)
         return cp(new(4, "U"), sub(B, 15, 64, 16)), NP, sub(GI, 0, 128, 2)
 
     for t in range(3):
@@ -459,46 +452,44 @@ def rank_program(g, core, T, topo):
                 mm(2 + b, E[b][0], E[b][1], *mov)
             mm(6, Wc, Ws, *mov)
             cp(ind(H, so), GI)
-            cp(ind(LOC, so), pos)
             vn = [tt(new(64), bank(h, 64, 128), NP, OP.subtract) for h in range(2)]
             for h in range(2):
                 cp(ind(V[h], so), vn[h])
             nf, off = new(2), new(2)
+            og = sub(OG, 2, 3) if t == 0 else sub(OG, 0, 2)
+            a = [act(new(16 + 16 * t), ind(sub(H, 0, 256), og), AF.Abs, bias=ngid[h]) for h in range(2)]
             for h in range(2):
-                a = act(new(256), sub(H, 0, 256), AF.Abs, bias=ngid[h])
-                act(new(256), a, AF.Relu, bias=k1, scale=-1.0, acc=sub(nf, h, h + 1))
+                act(new(16 + 16 * t), a[h], AF.Relu, bias=k1, scale=-1.0, acc=sub(nf, h, h + 1))
             act(off, nf, bias=kT, scale=-BIG)
             dma("y", T.ho[t:t + 1, :], mine(H))
 
             def later_s():
                 for b in range(4):
                     act(A("DW", W * b + 256 + 64 * t, W * b + 320 + 64 * t), bank(2 + b, 64, 128), AF.Copy, scale=0.5)
-            bids(t + 1, [sub(V[0], 0, 256), sub(V[1], 0, 256)], [sub(off, 0, 1), sub(off, 1, 2)], later_s)
+            bids(t + 1, [sub(V[0], 0, 256), sub(V[1], 0, 256)], [sub(off, 0, 1), sub(off, 1, 2)], later_s, lambda: cp(ind(LOC, so), pos))
             yn = act(new(64), bank(6, 64, 128), AF.Copy)
             cp(ind(P, so), NP)
             cp(ind(Y, so), yn)
             dma("y", T.pr[t:t + 1, :], mine(P))
         else:
             mm(6, Wc, Ws, *mov)
+            yn = act(new(64), bank(6, 64, 128), AF.Copy)
             cp(ind(LOC, so), pos)
-            cp(ind(H, so), GI)
-            lm = tt(new(32), sub(LOC, 32 * r, 32 * r + 32), MK, OP.mult)
-            cp(ind(P, so), NP)
+            cp(ind(Y, so), yn)
+            lm = tt(new(32), sub(LOC, 32 * r, 32 * r + 32), CM, OP.mult)
+            dma("y", T.y[:], sub(Y, 0, 256))
             l2 = new(2)
             for c in range(2):
                 red(sub(l2, c, c + 1), sub(lm, 16 * c, 16 * c + 16))
-            oo = ts(new(2, "U"), l2, wp, OP.subtract)
+            oo = ts(new(2, "U"), l2, 0.125, OP.mult, wp, OP.subtract)
+            pick(A("Oc", 0, 32), A("Os", 0, 32), *Vw(0, 448), oo)
+            dma("y", T.oc[:], A("Oc", 0, 32))
+            cp(ind(H, so), GI)
+            for q in range(4):
+                dma("sy"[q % 2], T.osc[4 * q:4 * q + 4, :], A("Os", 0, 32, 1, (32 * q, 32 * q + 4)))
+            cp(ind(P, so), NP)
             dma("s", T.ho[t:t + 1, :], mine(H))
             dma("y", T.pr[t:t + 1, :], mine(P))
-            yn = act(new(64), bank(6, 64, 128), AF.Copy)
-            pick(A("Oc", 0, 32), A("Os", 0, 32), *Vw(0, 448), oo)
-            cp(ind(Y, so), yn)
-            dma("y", T.oc[:], A("Oc", 0, 32))
-            for q in range(2):
-                dma("s", T.osc[4 * q:4 * q + 4, :], A("Os", 0, 32, 1, (32 * q, 32 * q + 4)))
-            dma("y", T.y[:], sub(Y, 0, 256))
-            for q in range(2, 4):
-                dma("sy"[q % 2], T.osc[4 * q:4 * q + 4, :], A("Os", 0, 32, 1, (32 * q, 32 * q + 4)))
 
     used = set()
     for o in ops:

@@ -1,26 +1,25 @@
 from concourse.bass import DstId, RemoteDMATransfer
 from concourse.mybir import dt, AluOpType as OP, AxisListType as AX, ActivationFunctionType as AF
 
-HELP = (3, 3, 3, 3)
+PAIR = (0, 1, 3)
 X4, U8 = "float8_e4m3fn_x4", "uint8"
 W = 384
 SCRATCH = {
-    "F": ("sbuf", [128, 24576], "float32"), "C": ("sbuf", [128, 4096], "float32"),
+    "F": ("sbuf", [128, 24576], "float32"), "C": ("sbuf", [128, 4096], "float32"), "N": ("sbuf", [128, 768], "bfloat16"),
     "U": ("sbuf", [128, 512], "uint16"), "L": ("sbuf", [128, 192], "float32"),
     "xb": ("sbuf", [128, 1024], "bfloat16"), "wb": ("sbuf", [128, 512], "bfloat16"), "Z": ("sbuf", [128, 520], "bfloat16"),
     "DX": ("sbuf", [128, 1024], "float32"), "DW": ("sbuf", [128, 4 * W], "float32"), "GX": ("sbuf", [128, 96], "float32"),
     "Xc": ("sbuf", [128, 256], X4), "Xs": ("sbuf", [128, 256], U8), "Pc": ("sbuf", [128, 256], X4), "Ps": ("sbuf", [128, 256], U8),
     "Wc": ("sbuf", [128, 128], X4), "Ws": ("sbuf", [128, 128], U8), "Ec": ("sbuf", [128, 512], X4), "Es": ("sbuf", [128, 512], U8),
     "Vc": ("sbuf", [128, 448], X4), "Vs": ("sbuf", [128, 448], U8), "Oc": ("sbuf", [128, 32], X4), "Os": ("sbuf", [128, 32], U8),
-    "T0": ("sbuf", [128, 512], "bfloat16"), "T1": ("sbuf", [128, 512], "bfloat16"),
+    "T0": ("sbuf", [128, 512], "bfloat16"), "T1": ("sbuf", [128, 576], "bfloat16"),
     "PS": ("psum", [128, 512 * 7], "float32"),
 }
 for _s in range(4):
-    SCRATCH["Sc%d" % _s] = ("sbuf", [128, 128], X4)
-    SCRATCH["Ss%d" % _s] = ("sbuf", [128, 128], U8)
-    SCRATCH["Hs%d" % _s] = ("sbuf", [128, 32], U8)
-SEMAPHORES = ["qv", "qs", "qt", "qg", "sent"] + ["d%d" % i for i in range(32)] + ["c%d" % i for i in range(4)] + ["l%d" % i for i in range(3)]
-
+    SCRATCH["Sc%d" % _s] = ("sbuf", [128, 256], X4)
+    SCRATCH["Ss%d" % _s] = ("sbuf", [128, 256], U8)
+SEMAPHORES = (["qv", "qs", "qt", "qg", "sent"] + ["d%d" % i for i in range(32)] + ["c%d" % i for i in range(4)]
+              + ["p%d" % i for i in range(4)] + ["l%d" % i for i in range(3)])
 BIG, TINY, PRED, MAG = 2.0 ** 96, 2.0 ** -90, 1.0 - 2.0 ** -24, 1.5 * 2.0 ** 23
 STAGE = ((32, 0), (8, 256), (8, 320), (8, 384))
 
@@ -33,49 +32,15 @@ def sub(v, a, b, s=1, p=None):
     return (v[0], v[1] + a, v[1] + b, s, v[4] if p is None else p[0], v[5] if p is None else p[1])
 
 
-def wiring(topo, cores, r):
-    core = cores[r]
-    sib = [q for q in range(8) if q != r and topo.chip(cores[q]) == topo.chip(core)][0]
-    off = [q for q in range(8) if topo.chip(cores[q]) != topo.chip(core)]
-    near = lambda q: topo.mates(topo.chip(core), topo.chip(cores[q])) or topo.same_plane(topo.chip(core), topo.chip(cores[q]))
-    off.sort(key=lambda q: (topo.die(cores[q]) == topo.die(core), near(q)))
-    aide = [c for c in topo.cores_of(core) if c not in cores and topo.die(c) == topo.die(core) and all(topo.may_write(c, cores[q]) for q in off)][0]
-    m_off = topo.mask(core, cores[off[0]])
-    return sib, off, aide, m_off, topo.mask(core, cores[sib]) & ~m_off
-
-
-def place(topo, c):
-    a = topo.addr(c)
-    return DstId(rid=int(a[0]), pnc=int(a[1]))
-
-
-def aide_program(g, core, T, topo):
-    cores = list(T.cores)
-    for r in range(8):
-        sib, off, aide, m_off, m_on = wiring(topo, cores, r)
-        if aide != core:
-            continue
-        sent = 0
-        for st, (n, base) in enumerate(STAGE):
-            if HELP[st]:
-                to = off[:HELP[st]]
-                g.wait_ge(T.sem["c%d" % st], bin(m_on).count("1"))
-                g.remote_dma_fused([RemoteDMATransfer(dst_ids=[place(topo, cores[q]) for q in to], dma_engine_mask=m_off, remote_sem=T.sem["c%d" % st],
-                                                      src=T["Hs%d" % st][:, 0:n], dsts=[T.Vs[:, base + n * r:base + n * r + n] for q in to])], local_sem=T.sem.sent)
-                sent += bin(m_off).count("1")
-        if sent:
-            g.wait_ge(T.sem.sent, sent)
-
-
 def rank_program(g, core, T, topo):
     r = T.rank_of(core)
     if r is None:
-        aide_program(g, core, T, topo)
         return
     cores = list(T.cores)
     ops, log = [], {}
     Q = {"v": g.vector, "s": g.scalar, "t": g.tensor, "g": g, "y": g.sync}
-    top = {"F": 0, "C": 0, "U": 0, "d": 0, "sent": 0}
+    top = {"F": 0, "C": 0, "U": 0, "N": 0, "d": 0, "sent": 0}
+    gv = g.vector
 
     def new(n, buf="F"):
         a = top[buf]
@@ -109,57 +74,28 @@ def rank_program(g, core, T, topo):
                 else:
                     touch(v, i, q, w, deps)
         ops.append({"q": q, "fn": fn, "deps": deps, "tok": tok})
+        return outs[0] if outs else None
 
     def ts(o, i, s1, op0, s2=None, op1=None):
         if op1 is None:
-            op("v", lambda: g.vector.tensor_scalar(ap(o), ap(i), ap(s1), None, op0), [o], [i, s1])
-        else:
-            op("v", lambda: g.vector.tensor_scalar(ap(o), ap(i), ap(s1), ap(s2), op0, op1), [o], [i, s1, s2])
-        return o
+            return op("v", lambda: gv.tensor_scalar(ap(o), ap(i), ap(s1), None, op0), [o], [i, s1])
+        return op("v", lambda: gv.tensor_scalar(ap(o), ap(i), ap(s1), ap(s2), op0, op1), [o], [i, s1, s2])
 
-    def tt(o, a, b, f):
-        op("v", lambda: g.vector.tensor_tensor(ap(o), ap(a), ap(b), f), [o], [a, b])
-        return o
-
-    def cp(o, i):
-        op("v", lambda: g.vector.tensor_copy(ap(o), ap(i)), [o], [i])
-        return o
-
-    def red(o, i, f=OP.add):
-        op("v", lambda: g.vector.tensor_reduce(ap(o), ap(i), AX.X, f), [o], [i])
-        return o
-
-    def scan(o, d0, d1, init, f0, f1):
-        op("v", lambda: g.vector.tensor_tensor_scan(ap(o), ap(d0), ap(d1), ap(init), f0, f1), [o], [d0, d1, init])
-        return o
-
-    def tr(o, i):
-        op("v", lambda: g.vector.transpose(ap(o), ap(i)), [o], [i])
-        return o
-
-    def ms(o, c):
-        op("v", lambda: g.vector.memset(ap(o), c), [o], [])
-        return o
+    tt = lambda o, a, b, f: op("v", lambda: gv.tensor_tensor(ap(o), ap(a), ap(b), f), [o], [a, b])
+    cp = lambda o, i: op("v", lambda: gv.tensor_copy(ap(o), ap(i)), [o], [i])
+    red = lambda o, i, f=OP.add: op("v", lambda: gv.tensor_reduce(ap(o), ap(i), AX.X, f), [o], [i])
+    scan = lambda o, d0, d1, init, f0, f1: op("v", lambda: gv.tensor_tensor_scan(ap(o), ap(d0), ap(d1), ap(init), f0, f1), [o], [d0, d1, init])
+    tr = lambda o, i: op("v", lambda: gv.transpose(ap(o), ap(i)), [o], [i])
+    ms = lambda o, c: op("v", lambda: gv.memset(ap(o), c), [o], [])
+    quant = lambda c, s, i: op("v", lambda: gv.quantize_mx(ap(c), ap(s), ap(i)), [c, s], [i])
 
     def act(o, i, f=AF.Identity, bias=None, scale=None, acc=None):
-        def fn():
-            k = {}
-            if bias is not None:
-                k["bias"] = ap(bias)
-            if scale is not None:
-                k["scale"] = ap(scale)
-            if acc is not None:
-                k["accum_out"] = ap(acc)
-            return g.scalar.activation(ap(o), ap(i), f, **k)
-        op("s", fn, [o, acc], [i, bias, scale])
-        return o
+        k = [(n, v) for n, v in (("bias", bias), ("scale", scale), ("accum_out", acc)) if v is not None]
+        return op("s", lambda: g.scalar.activation(ap(o), ap(i), f, **{n: ap(v) for n, v in k}), [o, acc], [i, bias, scale])
 
     def ssum(o, i):
         act(new(i[2] - i[1]), i, acc=o)
         return o
-
-    def quant(c, s, i):
-        op("v", lambda: g.vector.quantize_mx(ap(c), ap(s), ap(i)), [c, s], [i])
 
     def mm(bank, lc, ls, rc, rs):
         o = A("PS", 512 * bank, 512 * bank + rc[2] - rc[1])
@@ -171,8 +107,7 @@ def rank_program(g, core, T, topo):
             for s, c in pat:
                 n *= c
             o = new(n, "C")
-        op("g", lambda: g.iota(ap(o), pat, base, cm, allow_small_or_imprecise_dtypes=True), [o], [])
-        return o
+        return op("g", lambda: g.iota(ap(o), pat, base, cm, allow_small_or_imprecise_dtypes=True), [o], [])
 
     def raw(v):
         if isinstance(v, tuple) and SCRATCH[v[0]][2] == X4:
@@ -185,19 +120,29 @@ def rank_program(g, core, T, topo):
         op(q, lambda: Q[q].dma_start(raw(o), raw(i)).then_inc(T.sem[sem], 16), [o], [i], (sem, 16))
 
     def pick(oc, os, wc, ws, off):
-        op("v", lambda: g.vector.tensor_copy(ap(oc).bitcast(dt.uint32), ap(wc).bitcast(dt.uint32).indirect(ap(off))), [oc], [wc, off])
+        op("v", lambda: gv.tensor_copy(ap(oc).bitcast(dt.uint32), ap(wc).bitcast(dt.uint32).indirect(ap(off))), [oc], [wc, off])
         act(os, ("ind", ws, off), AF.Copy)
 
-    sib, off_chip, aide, m_off, m_on = wiring(topo, cores, r)
+    sib = [q for q in range(8) if q != r and topo.chip(cores[q]) == topo.chip(core)][0]
     assert sib == r ^ 1
     u = r % 2
+    off_chip = [q for q in range(8) if topo.chip(cores[q]) != topo.chip(core)]
+    off_chip.sort(key=lambda q: (topo.die(cores[q]) == topo.die(core), topo.same_plane(topo.chip(core), topo.chip(cores[q])),
+                                 topo.mates(topo.chip(core), topo.chip(cores[q]))))
+    far = [q for q in off_chip if topo.die(cores[q]) == topo.die(core)]
+    m_off = topo.mask(core, cores[off_chip[0]])
+    m_on = topo.mask(core, cores[sib]) & ~m_off
     n_off, n_on = bin(m_off).count("1"), bin(m_on).count("1")
 
-    def call(parts, sem):
+    def dst(q):
+        a = topo.addr(cores[q])
+        return DstId(rid=int(a[0]), pnc=int(a[1]))
+
+    def call(parts):
         def fn():
-            return g.remote_dma_fused([RemoteDMATransfer(dst_ids=[place(topo, c) for c, d in to], dma_engine_mask=m, remote_sem=T.sem[sem],
-                                                         src=raw(s), dsts=[raw(d) for c, d in to]) for s, to, m in parts], local_sem=T.sem.sent)
-        top["sent"] += sum(bin(p[2]).count("1") for p in parts)
+            return g.remote_dma_fused([RemoteDMATransfer(dst_ids=[dst(q) for q in to], dma_engine_mask=m, remote_sem=T.sem[sem],
+                                                         src=raw(s), dsts=[raw(d) for q in to]) for s, d, to, m, sem in parts], local_sem=T.sem.sent)
+        top["sent"] += sum(bin(p[3]).count("1") for p in parts)
         op("g", fn, [], [p[0] for p in parts], ("none", 0))
 
     def arrive(views, sem, count):
@@ -206,101 +151,119 @@ def rank_program(g, core, T, topo):
 
     def share_cols(st):
         n, base = STAGE[st]
-        lo, hi, a = base + n * r, base + n * (r + 1), max(st - 1, 0) * n
-        sc, ss, vc, vs = A("Sc%d" % st, a, a + n), A("Ss%d" % st, a, a + n), A("Vc", lo, hi), A("Vs", lo, hi)
-        sem = arrive([A(v, x, y) for v in ("Vc", "Vs") for x, y in ((base, lo), (hi, base + 8 * n)) if x < y], "c%d" % st, 2 * (n_off * len(off_chip) + n_on))
-        to = lambda qs, d: [(cores[q], d) for q in qs]
-        call([(ss, [(aide, A("Hs%d" % st, 0, n))] + to([sib], vs), m_on), (ss, to(off_chip[HELP[st]:], vs), m_off)], sem)
-        call([(sc, to(off_chip, vc), m_off), (sc, to([sib], vc), m_on)], sem)
+        lo, hi, a, pl = base + n * r, base + n * (r + 1), 128 - n + n * u, base + n * (r - u)
+        sc, vc, ss, vs = A("Sc%d" % st, a, a + n), A("Vc", lo, hi), A("Ss%d" % st, a, a + n), A("Vs", lo, hi)
+        rest = lambda v, x0, x1: [A(v, x, y) for x, y in ((base, x0), (x1, base + 8 * n)) if x < y]
+        if st not in PAIR:
+            sem = arrive(rest("Vc", lo, hi) + rest("Vs", lo, hi), "c%d" % st, 2 * (n_off * len(off_chip) + n_on))
+            for s, d in ((sc, vc), (ss, vs)):
+                call([(s, d, off_chip, m_off, sem), (s, d, [sib], m_on, sem)])
+                dma("y", d, s)
+            return lambda: None
+        sem = arrive(rest("Vc", lo, hi) + rest("Vs", pl, pl + 2 * n), "c%d" % st, n_off * (len(off_chip) + len(far)) + n_on)
+        k = 4 * n if st else n
+        wide = lambda who: A("Ss%d" % st, 128 - k + k * who, 128 + k * who)
+        first = (wide(u), wide(u), [sib], m_on, arrive([wide(1 - u)], "p%d" % st, n_on))
+        codes = [(sc, vc, off_chip, m_off, sem), (sc, vc, [sib], m_on, sem)]
+        for parts in ([codes[0], first], codes[1:]) if st else ([first], codes):
+            call(parts)
         dma("y", vc, sc)
-        dma("y", vs, ss)
+
+        def hand_on():
+            pair, vp = A("Ss%d" % st, 128 - n, 128 + n), A("Vs", pl, pl + 2 * n)
+            call([(pair, vp, far, m_off, sem)])
+            dma("y", vp, pair)
+        return hand_on
 
     def share_list(t):
         b = 64 * t + 8 * (r - u)
         own, oth = A("L", b + 3 + 5 * u, b + 8 + 5 * u), A("L", b + 8 - 5 * u, b + 13 - 5 * u)
         rest = [A("L", x, y) for x, y in ((64 * t, b), (b + 16, 64 * t + 64)) if x < y]
-        call([(own, [(cores[q], own) for q in off_chip], m_off), (own, [(cores[sib], own)], m_on)],
-             arrive(rest + [oth], "l%d" % t, n_off * len(off_chip) + n_on))
+        sem = arrive(rest + [oth], "l%d" % t, n_off * len(off_chip) + n_on)
+        call([(own, own, off_chip, m_off, sem), (own, own, [sib], m_on, sem)])
 
     def quant_stage(st):
-        quant(A("Sc%d" % st, 0, 128), A("Ss%d" % st, 0, 128), A("T%d" % min(st, 1), 0, 512))
+        a = 32 * max(st - 1, 0)
+        quant(A("Sc%d" % st, 128 * u, 128 * u + 128), A("Ss%d" % st, 128 * u, 128 * u + 128), A("T%d" % min(st, 1), a, a + 512))
 
-    dma("y", A("T0", 0, 128), T.it[:])
+    dma("y", A("T0", 384 - 384 * u, 512 - 384 * u), T.it[:])
     dma("y", A("xb", 0, 1024), T.x[:])
     dma("y", A("wb", 0, 512), T.w[:])
-    RW = new(256, "C")
-    for i, (pat, base) in enumerate((([[1, 32]], 0), ([[0, 2], [1, 16]], 0), ([[0, 8], [256, 4]], -256 * r), ([[0, 8], [W, 4]], 0),
-                                     ([[0, 2], [2, 4], [0, 4]], 1), ([[5, 2], [0, 16]], 3), ([[0, 4], [1, 8]], 0), ([[0, 4], [16, 4], [5, 2]], 7))):
-        iota(sub(RW, 32 * i, 32 * i + 32), pat, base)
-    ms(A("T0", 128, 512), 0.0)
+    ID = iota(None, [[1, 128]], 0, -1)
+    RW = new(192, "C")
+    for i, pat in enumerate(([[1, 32]], [[0, 2], [1, 16]], [[0, 8], [1, 4]], [[0, 2], [1, 4], [0, 4]])):
+        iota(sub(RW, 32 * i, 32 * i + 32), pat)
+    xo = iota(None, [[32, 2], [64, 4], [16, 2]])
+    ms(A("T0", 128 * u, 384 + 128 * u), 0.0)
     LM = ms(A("L", 0, 192), 0.0)
+    ms(A("Z", 0, 516), 0.0)
+    CB = [8192.0 * (256 + 64 * t + 8 * r) for t in range(3)]
     cst = new(16, "C")
-    for i, c in enumerate((TINY, -32767.5 / 65536, MAG, -MAG * 32768, -TINY, 1.0, 256.0, -1.0, PRED, -256.0, -0.25, 0.25)):
+    for i, c in enumerate([TINY, MAG, -MAG * 32768, MAG * 8192, -TINY, 1.0, 256.0] + [(-32767.5 - c) / 65536 for c in CB]):
         ms(sub(cst, i, i + 1), c)
-    kT, kO, kM, kM15, kN, k1, k256, km1, kP, km256, kmq, kq = [sub(cst, i, i + 1) for i in range(12)]
+    kT, kM, kM15, kM13, kN, k1, k256 = [sub(cst, i, i + 1) for i in range(7)]
+    kO = [sub(cst, 7 + t, 8 + t) for t in range(3)]
+    ts(A("Z", 3, 515, 4), ID, 0.0, OP.is_equal)
     op("g", None, [], [LM], ("none", 0))
     quant_stage(0)
-    share_cols(0)
-    IO = iota(None, [[1, 516]])
-    p43, xo, p2 = iota(None, [[1, 1]], 3, 4), iota(None, [[32, 2], [64, 4], [16, 2]]), iota(None, [[32, 2]], 256 * r, 2)
+    hand_on = share_cols(0)
     MP = new(224, "C")
-    for i, (pat, base) in enumerate((([[1000, 4], [1, 8]], -1000 * (r % 4)), ([[0, 2], [1, 8], [1000, 2]], 0), ([[0, 2], [1, 4], [0, 4]], 0),
-                                     ([[0, 2], [1, 4], [0, 4]], 4), ([[0, 2], [1, 8], [-1000, 2]], 1000))):
+    p2, mq = iota(None, [[32, 2]], 256 * r, 2), iota(None, [[1024, 4], [1, 8]], 0, -32)
+    for i, pat, base in ((0, [[1000, 4], [1, 8]], -1000 * (r % 4)), (1, [[0, 2], [1, 8], [1000, 2]], 0), (4, [[0, 2], [1, 8], [-1000, 2]], 1000)):
         iota(sub(MP, 32 * i, 32 * i + 32), pat, base)
-    mq, gb, trs = iota(None, [[1024, 4], [1, 8]], 0, -32), iota(None, [[16, 4], [0, 2]]), iota(None, [[16, 4], [-1000, 16]], 256)
-    P = ms(new(320), 0.0)
-    Xc, Xs = A("Xc", 0, 256), A("Xs", 0, 256)
-    quant(Xc, Xs, A("xb", 0, 1024))
-    RT = tr(new(256, "C"), RW)
-    p32, p16, xadd, wp, lk, par, p8, gw = [sub(RT, 32 * i, 32 * i + 1) for i in range(8)]
-    Wc, Ws = A("Wc", 0, 128), A("Ws", 0, 128)
-    quant(Wc, Ws, A("wb", 0, 512))
-    CT = new(96, "C")
-    ms(sub(CT, 0, 32), PRED)
-    ms(sub(CT, 64, 96), 1.0)
-    ms(A("T1", 0, 512), 0.0)
-    ts(A("Z", 0, 516), IO, p43, OP.is_equal)
-    XP = ts(new(16, "U"), xo, p16, OP.add)
+    hand_on()
+    H = iota(new(320), [[8192, 320]], -1)
+    for i, pat, base in ((4, [[0, 4], [1, 8]], 0), (5, [[0, 4], [16, 4], [5, 2]], 7)):
+        iota(sub(RW, 32 * i, 32 * i + 32), pat, base)
+    gb, trs = iota(None, [[16, 4], [0, 2]], 3), iota(None, [[16, 4], [-1000, 16]], 256)
+    H2 = iota(new(320), [[2048, 320]])
     E = [(A("Ec", 128 * b, 128 * b + 128), A("Es", 128 * b, 128 * b + 128)) for b in range(4)]
     for b in range(4):
         quant(E[b][0], E[b][1], A("Z", 3 - b, 515 - b))
+    Xc, Xs = A("Xc", 0, 256), A("Xs", 0, 256)
+    RT = tr(new(128, "C"), sub(RW, 0, 128))
+    quant(Xc, Xs, A("xb", 0, 1024))
+    p32, p16, p4, q4 = [sub(RT, 32 * i, 32 * i + 1) for i in range(4)]
+    XP = ts(new(16, "U"), xo, p16, OP.add)
+    P = ms(new(320), 0.0)
     pick(A("Pc", 0, 256), A("Ps", 0, 256), Xc, Xs, XP)
     for b in range(4):
         mm(2 + b, E[b][0], E[b][1], Xc, Xs)
     for b in range(4):
         act(A("DX", 256 * b, 256 * b + 256), A("PS", 512 * (2 + b), 512 * (2 + b) + 256), AF.Copy, scale=0.5)
-    t0 = ts(new(32, "C"), sub(IO, 0, 32), p32, OP.is_gt, 2.0 ** -24, OP.mult)
-    ML = ts(new(16, "C"), sub(RW, 192, 208), lk, OP.is_equal)
-    CM = ts(new(32, "C"), sub(RW, 32, 64), p16, OP.is_equal, 8.0, OP.mult)
-    TRI = ts(sub(CT, 32, 64), t0, PRED, OP.add)
-    sl = tr(new(32, "C"), sub(MP, 128, 160))
-    GA = ts(new(8, "U"), gb, par, OP.add)
-    GB = ts(new(8, "U"), gb, par, OP.add, 4.0, OP.add)
-    GW = cp(new(1, "U"), gw)
-    slot = ts(new(1, "C"), sub(sl, 0, 1), 8.0, OP.is_lt, sub(sl, 0, 1), OP.mult)
-    gid2 = ts(new(2, "C"), p2, p32, OP.subtract)
-    gid = [sub(gid2, h, h + 1) for h in range(2)]
+    Wc, Ws = A("Wc", 0, 128), A("Ws", 0, 128)
+    quant(Wc, Ws, A("wb", 0, 512))
+    CT = new(96, "C")
+    ms(sub(CT, 32, 64), PRED)
+    ms(sub(CT, 64, 96), 1.0)
+    ms(A("T1", 0, 576), 0.0)
+    t0 = ts(new(32, "C"), sub(RW, 0, 32), p32, OP.is_gt, 2.0 ** -24, OP.mult)
     q32 = ts(new(1, "C"), p32, 32.0, OP.mult)
+    wq = ts(new(1, "C"), p4, float(W), OP.mult, 0.25, OP.add)
+    xadd = ts(new(1, "C"), p4, 256.0, OP.mult, -256.0 * r, OP.add)
+    TRI = ts(sub(CT, 0, 32), t0, PRED, OP.add)
+    cp(sub(MP, 64, 96), sub(RW, 96, 128))
+    ts(sub(MP, 96, 128), sub(RW, 96, 128), 4.0, OP.add)
+    RS = ts(new(16, "C"), sub(RW, 0, 16), 8.0, OP.not_equal)
+    gid2 = ts(new(2, "C"), p2, p32, OP.subtract)
+    mapQ = ts(new(32, "C"), mq, q32, OP.add)
     cp(sub(MP, 160, 192), sub(MP, 0, 32))
     cp(sub(MP, 192, 224), sub(MP, 128, 160))
-    mapQ = ts(new(32, "C"), mq, q32, OP.add)
-    ngid2 = ts(new(2, "C"), gid2, -1.0, OP.mult)
-    ngid = [sub(ngid2, h, h + 1) for h in range(2)]
-    ntr = [ts(new(1, "C"), p32, -1.0, OP.mult, -256.0 - 32 * b, OP.add) for b in range(2)]
-    kb1, kb2 = ts(new(1, "C"), p8, -32.0, OP.add, 1.0 / 128, OP.mult), ts(new(1, "C"), p8, 4096.0, OP.add, 1.0 / 16384, OP.mult)
-    TRS = ts(new(64, "C"), trs, p16, OP.add)
-    LOC = act(new(320), sub(IO, 0, 320), bias=wp)
-    IW = act(new(192, "C"), sub(IO, 256, 448), bias=wp)
-    H = act(new(320), P, bias=km1)
+    gid = [ts(new(2, "C"), gid2, c, OP.add) for c in CB]
+    ML = new(16, "C")
+    for c in range(2):
+        ts(sub(ML, 8 * c, 8 * c + 8), sub(MP, 128 + 8 * c, 136 + 8 * c), -4.0 * c, OP.add, q4, OP.is_equal)
 
     V = [new(320), new(320)]
     Y = new(320)
+    PW = new(448)
     OG = new(4, "U")
     bank = lambda b, lo, hi: A("PS", 512 * b + lo, 512 * b + hi)
     Vw = lambda a, b: (A("Vc", a, b), A("Vs", a, b))
     Xp = lambda h: (A("Pc", 128 * h, 128 * h + 128), A("Ps", 128 * h, 128 * h + 128))
     ind = lambda w, o: ("ind", w, o)
     mine = lambda v: sub(v, 32 * r, 32 * r + 32, 1, (0, 1))
+    one = lambda v: sub(v, 0, v[2] - v[1], 1, (0, 1))
 
     def bids(t, src, off, later_s, after_list):
         Fs, Ss, goal, gi, key = [new(256), new(256)], [new(256), new(256)], new(2), new(2), new(2)
@@ -309,20 +272,20 @@ def rank_program(g, core, T, topo):
         for h in range(2):
             scan(Fs[h], src[h], src[h] if t else sub(P, 0, 256), -BIG, OP.max, OP.max if t else OP.add)
             act(new(256), Fs[h], AF.Sign, bias=sub(Fs[h], 255, 256), scale=-1.0, acc=sub(goal, h, h + 1))
+        for h in range(2):
             scan(sub(Ss[h], 0, 255), sub(src[h], 1, 256), sub(Fs[h], 0, 255), -BIG, OP.max, OP.min)
-            if h == 0:
-                act(k[0], act(new(1), sub(Ss[0], 254, 255), bias=sub(Fs[0], 255, 256), scale=-1.0), bias=off[0])
-                act(sub(B, 32, 96), sub(CT, 32, 96), scale=k[0])
+        act(k[0], act(new(1), sub(Ss[0], 254, 255), bias=sub(Fs[0], 255, 256), scale=-1.0), bias=off[0])
+        act(sub(B, 0, 32), sub(CT, 64, 96), scale=k[0])
+        act(sub(B, 96, 128), TRI, scale=k[0])
         ts(k[1], sub(Fs[1], 255, 256), sub(Ss[1], 254, 255), OP.subtract, off[1], OP.add)
         for h in range(2):
-            act(sub(gi, h, h + 1), sub(goal, h, h + 1), bias=gid[h], scale=2048.0)
+            act(sub(gi, h, h + 1), sub(goal, h, h + 1), bias=sub(gid[t], h, h + 1), scale=2048.0)
         later_s()
-        ts(sub(B, 0, 32), sub(CT, 0, 32), k[1], OP.mult)
-        ts(sub(B, 96, 128), TRI, k[1], OP.mult)
+        ts(sub(B, 32, 96), sub(CT, 0, 64), k[1], OP.mult)
         B = tr(new(128), B)
         G, rk = new(128), [new(1), new(1)]
         for h in (1, 0):
-            ts(sub(G, 64 * h, 64 * h + 64), sub(B, 64 * h, 64 * h + 64), k[h], OP.is_ge)
+            ts(sub(G, 64 * h, 64 * h + 64), sub(B, 64 - 64 * h, 128 - 64 * h), k[h], OP.is_ge)
         (ssum if t else red)(rk[1], sub(G, 64, 128))
         red(rk[0], sub(G, 0, 64))
         O = new(128)
@@ -337,8 +300,8 @@ def rank_program(g, core, T, topo):
             tt(sub(P2, 0, 2, 1, (a, a + 32)), sub(P1, 63, 128, 64, (0, 32)), sub(P1, 63, 128, 64, (32, 64)), OP.add)
         ck, cg = sub(P2, 0, 1), sub(P2, 1, 2)
         B = ts(new(32), TRI, ck, OP.mult)
-        y = ts(new(1), cg, -1023.5, OP.add, 2.0 ** -11, OP.mult)
-        n = act(new(1), cg, bias=kO, scale=2.0 ** -16)
+        y = ts(new(1), cg, -1023.5 - CB[t], OP.add, 2.0 ** -11, OP.mult)
+        n = act(new(1), cg, bias=kO[t], scale=2.0 ** -16)
         n = act(new(1), n, bias=kM)
         n = act(new(1), n, bias=kM15, scale=32768.0)
         B = tr(new(32), B)
@@ -348,148 +311,182 @@ def rank_program(g, core, T, topo):
         r2 = red(new(1), B)
         cc = act(new(1), gs, bias=n)
         gd = ts(new(1), gl, -2048.0, OP.mult, cg, OP.add)
-        O = new(288)
+        O, Ot = new(288), new(288)
         oh = lambda a, b, m, pay: ts(sub(O, a, b), sub(MP, m, m + b - a), r2, OP.is_equal, pay, OP.mult)
+        e = 288 if t + 1 in PAIR else 224
         oh(0, 64, 0, ck)
         oh(128, 192, 160, gl)
+        oh(192, e, 32, gd)
         oh(64, 128, 128, cc)
-        oh(192, 288, 32, gd)
-        Ot = new(288)
-        tr(sub(Ot, 0, 224), sub(O, 0, 224))
+        tr(sub(Ot, 0, e), sub(O, 0, e))
         m = 64 * t + 8 * (r - u) + 3 + 5 * u
         col = lambda f: A("L", m + f, m + f + 1)
         blk = lambda a, b: sub(Ot, 32 * a, 32 * b)
         ssum(col(1), blk(0, 1))
-        red(col(0), blk(1, 3))
         red(col(4), blk(5, 7))
+        red(col(0), blk(1, 3))
         ssum(col(3), blk(4, 5))
         red(col(2), blk(3, 4))
         share_list(t)
+        if e < 288:
+            oh(224, 288, 64, gd)
         og = ts(sub(OG, 2, 3) if t == 0 else sub(OG, 0, 1) if t == 1 else new(1, "U"), col(4), 255.0, OP.min)
-        tr(sub(Ot, 224, 288), sub(O, 224, 288))
+        if e < 288:
+            tr(sub(Ot, 224, 288), sub(O, 224, 288))
         after_list()
-        l2, x2 = new(2), new(2)
+        x2 = new(2)
         for c in range(2):
             ssum(sub(x2, c, c + 1), blk(7 + c, 8 + c))
-        lr = tt(new(16), ind(LOC, og), ML, OP.mult)
-        ox = ts(new(2, "U"), x2, xadd, OP.add)
-        for c in range(2):
-            red(sub(l2, c, c + 1), sub(lr, 8 * c, 8 * c + 8))
+        lr = tt(new(16), ind(H, og), ML, OP.mult)
+        ox = ts(new(2, "U"), x2, -CB[t], OP.add, xadd, OP.add)
+        l2 = scan(new(16), RS, lr, 0.0, OP.mult, OP.add)
         gx = act(A("GX", 32 * t, 32 * t + 32), ind(A("DX", 0, 1024), ox), AF.Copy)
-        ov = cp(new(2, "U"), l2)
-        tt(A("T1", 32 * t, 32 * t + 32), ind(A("DW", 0, 256 + 64 * t + 3 * W), ov), gx, OP.add)
+        ov = ts(new(2, "U"), sub(l2, 7, 16, 8), 2.0 ** -13, OP.mult, wq, OP.add)
+        tt(A("T1", 32 * t + 480 - 480 * u, 32 * t + 512 - 480 * u), ind(A("DW", 0, 256 + 64 * t + 3 * W), ov), gx, OP.add)
         quant_stage(t + 1)
-        share_cols(t + 1)
+        share_cols(t + 1)()
         if t == 0:
             cp(sub(OG, 1, 2), og)
+        return gi
 
     for h in range(2):
         mm(h, *Xp(h), *Vw(0, 256))
     for b in range(4):
         mm(2 + b, E[b][0], E[b][1], *Vw(0, 256))
     mm(6, Wc, Ws, *Vw(0, 256))
-    act(sub(V[1], 0, 256), bank(1, 0, 256), AF.Copy)
 
     def first_s():
         for b in range(4):
             act(A("DW", W * b, W * b + 256), bank(2 + b, 0, 256), AF.Copy, scale=0.5)
-    bids(0, [bank(0, 0, 256), sub(V[1], 0, 256)], [kT, kT], first_s, lambda: None)
-    act(sub(V[0], 0, 256), bank(0, 0, 256), AF.Copy)
+    gi = bids(0, [bank(0, 0, 256), bank(1, 0, 256)], [kT, kT], first_s, lambda: None)
+    for h in range(2):
+        act(sub(V[h], 0, 256), bank(h, 0, 256), AF.Copy)
     act(sub(Y, 0, 256), bank(6, 0, 256), AF.Copy)
+    act(sub(PW, 0, 256), sub(P, 0, 256), AF.Copy)
+
+    sl = tr(new(32, "C"), sub(MP, 128, 160))
+    se = tr(new(32, "C"), sub(MP, 32, 64))
+    RT = tr(new(64, "C"), sub(RW, 128, 192))
+    par = ts(new(1, "C"), p32, p16, OP.subtract, 5.0 / 16, OP.mult)
+    p8, gw = sub(RT, 0, 1), sub(RT, 32, 33)
+    slot = ts(new(1, "C"), sub(sl, 0, 1), 8.0, OP.is_lt, sub(sl, 0, 1), OP.mult)
+    slotw = ts(new(1, "C"), sub(se, 0, 1), 8.0, OP.is_lt, sub(se, 0, 1), OP.mult)
+    GA = ts(new(8, "U"), gb, par, OP.add)
+    GB = ts(new(8, "U"), gb, par, OP.add, 4.0, OP.add)
+    GW = cp(new(1, "U"), gw)
+    CM = ts(new(32, "C"), sub(RW, 32, 64), p16, OP.is_equal, 8.0, OP.mult)
+    SR, GM = ts(new(32, "C"), sub(RW, 128, 160), 8192.0, OP.mult), []
+    slotw = ts(new(1, "C"), slotw, 8192.0, OP.mult)
+    ntr = new(2, "C")
+    for b in range(2):
+        ts(sub(ntr, b, b + 1), p32, -1.0, OP.mult, -256.0 - 32 * b, OP.add)
+    kb1, kb2 = ts(new(1, "C"), p8, -32.0, OP.add, 1.0 / 128, OP.mult), ts(new(1, "C"), p8, 4096.0, OP.add, 1.0 / 16384, OP.mult)
+    TRS = ts(new(64, "C"), trs, p16, OP.add)
+    R16 = ts(new(32, "C"), sub(RW, 0, 32), 16.0, OP.not_equal)
+    PR = new(32, "C")
+    for c in range(2):
+        ts(sub(PR, 16 * c, 16 * c + 16), sub(MP, 128, 144), 8192.0, OP.mult, CB[1 - c], OP.add)
 
     def sales(t):
         L = A("L", 64 * t, 64 * t + 64)
         t1 = tt(new(48), sub(L, 0, 48), sub(L, 16, 64), OP.add)
-        GI = act(new(128), ind(L, GB), AF.Copy)
-        IN = ts(new(128), ind(L, GA), slot, OP.add)
-        ow = tt(new(37), sub(t1, 3, 40), sub(t1, 8, 45), OP.add)
+        IN = act(new(128), ind(L, GA), bias=slot)
+        lo, hi = (0, 64), (64, 128)
+        ow = new(2)
+        for b, p in enumerate((lo, hi)):
+            tt(sub(ow, 0, 2, 1, p), sub(t1, 4 + 32 * b, 6 + 32 * b, 1, p), sub(t1, 9 + 32 * b, 11 + 32 * b, 1, p), OP.add)
         R = tr(new(128), IN)
         K, G = sub(R, 0, 128, 2), sub(R, 1, 128, 2)
-        k, gl = [[sub(ow, 32 * b + f, 32 * b + f + 1) for b in range(2)] for f in (1, 3)]
-        b1 = act(new(2), sub(ow, 2, 35, 32), bias=kb1, scale=1.0 / 128)
-        b2 = act(new(2), sub(ow, 2, 35, 32), bias=kb2, scale=1.0 / 16384)
-        half = lambda v, b: sub(v, 64 * b, 64 * b + 64)
-        S, Q1, Q2, X1, X2, Wn = [new(128) for i in range(6)]
-        for b in range(2):
-            act(half(S, b), K, AF.Sign, bias=k[b], scale=-1.0)
-            act(half(Q1, b), G, AF.Square, bias=sub(b1, b, b + 1), scale=-1.0 / 128)
-        for b in range(2):
-            act(half(Q2, b), G, AF.Square, bias=sub(b2, b, b + 1), scale=-1.0 / 16384)
-        GI = tr(new(128), GI)
+        b1 = act(new(1), sub(ow, 1, 2), bias=kb1, scale=1.0 / 128)
+        b2 = act(new(1), sub(ow, 1, 2), bias=kb2, scale=1.0 / 16384)
+        S = act(new(64), K, AF.Sign, bias=sub(ow, 0, 1), scale=-1.0)
+        Q1 = act(new(64), G, AF.Square, bias=b1, scale=-1.0 / 128)
+        Q2 = act(new(64), G, AF.Square, bias=b2, scale=-1.0 / 16384)
+        GI = ts(new(128), ind(L, GB), slotw, OP.add)
+        X1 = tt(new(64), S, Q1, OP.add)
         if t:
             po = ts(new(16, "U"), ind(L, GW), 255.0, OP.min)
-        for b in range(2):
-            tt(half(X1, b), half(S, b), half(Q1, b), OP.add)
-        best = [red(new(1), half(X1, b), OP.min) for b in range(2)]
-        gm = [act(new(1), gl[b], bias=ntr[b]) for b in range(2)]
-        lose = [act(new(1), best[b], bias=k256, scale=-4096.0) for b in range(2)]
-        NP = act(new(64), K, bias=kN)
+        best = red(new(1), X1, OP.min)
+        pw = sub(PW, 256 + 64 * t, 320 + 64 * t)
+        NP = act(new(64) if t else pw, K, bias=kN)
+        lose = act(new(1), best, bias=k256, scale=-4096.0)
         if t:
             PG = act(new(128), ind(P, sub(po, 0, 8)), AF.Copy)
-        for b in range(2):
-            tt(half(X2, b), half(Q2, b), half(S, b), OP.subtract)
-        for b in range(2):
-            ts(half(Wn, b), half(X2, b), 0.06, OP.max, best[b], OP.is_lt)
-        Wn = tr(new(128), Wn)
-        cn = [scan(new(32), sub(Wn, 32 * b, 32 * b + 32), sub(Wn, 64 + 32 * b, 96 + 32 * b), lose[b], OP.add, OP.add) for b in range(2)]
+        X2 = tt(new(64), Q2, S, OP.subtract)
+        Wn = ts(new(64, "N"), X2, 0.06, OP.max, best, OP.is_lt)
+        gl = tt(new(2), sub(t1, 6, 39, 32), sub(t1, 11, 44, 32), OP.add)
+        Wn = tr(new(64, "N"), Wn)
+        gm = tt(new(2), gl, ntr, OP.add)
+        cn = [new(32), new(32)]
+        for b, (own, oth) in enumerate(((lo, hi), (hi, lo))):
+            for p in (lo, hi):
+                scan(sub(cn[b], 0, 32, 1, p), sub(Wn, 32 * b, 32 * b + 32, 1, own), sub(Wn, 32 * b, 32 * b + 32, 1, oth), sub(lose, 0, 1, 1, own), OP.add, OP.add)
         B = new(64)
         for b in range(2):
-            ts(sub(B, 32 * b, 32 * b + 32), CM, sub(cn[b], 31, 32), OP.is_gt, gm[b], OP.mult)
+            ts(sub(B, 32 * b, 32 * b + 32), CM, sub(cn[b], 31, 32), OP.is_gt, sub(gm, b, b + 1), OP.mult)
         B = tr(new(64), B)
+        GI = tr(new(128), GI)
         B = scan(new(64), TRS, B, 0.0, OP.max, OP.add)
         if t:
-            NP = tt(new(64), sub(PG, 1, 128, 2), NP, OP.add)
+            NP = tt(pw, sub(PG, 1, 128, 2), NP, OP.add)
+        else:
+            GM.append(tt(new(32), sub(GI, r // 4 * 64, r // 4 * 64 + 64, 2), SR, OP.subtract))
         return cp(new(4, "U"), sub(B, 15, 64, 16)), NP, sub(GI, 0, 128, 2)
+
+    def holders(t, q):
+        a = act(one(new(32)), mine(H), bias=one(kM), scale=2.0 ** -13)
+        a = act(one(new(32)), a, bias=one(kM13), scale=-8192.0)
+        return lambda: dma(q, T.ho[t:t + 1, :], tt(one(new(32)), a, mine(H), OP.add))
 
     for t in range(3):
         so, NP, GI = sales(t)
         mov = Vw(192 + 64 * t, 320 + 64 * t)
-        pos = sub(IW, 64 * t, 64 * t + 64)
         if t < 2:
             for h in range(2):
                 mm(h, *Xp(h), *mov)
             for b in range(4):
                 mm(2 + b, E[b][0], E[b][1], *mov)
             mm(6, Wc, Ws, *mov)
-            cp(ind(H, so), GI)
+            if t:
+                cp(ind(H, so), GI)
+                hg = tt(new(32), ind(sub(H, 0, 256), sub(OG, 0, 2)), PR, OP.subtract)
+            else:
+                hg = tt(new(32), ind(H2, sub(so, r // 4 * 2, r // 4 * 2 + 2)), GM[0], OP.add)
             vn = [tt(new(64), bank(h, 64, 128), NP, OP.subtract) for h in range(2)]
             for h in range(2):
                 cp(ind(V[h], so), vn[h])
             nf, off = new(2), new(2)
-            og = sub(OG, 2, 3) if t == 0 else sub(OG, 0, 2)
-            a = [act(new(16 + 16 * t), ind(sub(H, 0, 256), og), AF.Abs, bias=ngid[h]) for h in range(2)]
+            a = [act(new(32), hg, AF.Abs, bias=sub(gid2 if t else gi, h, h + 1), scale=-1.0) for h in range(2)]
             for h in range(2):
-                act(new(16 + 16 * t), a[h], AF.Relu, bias=k1, scale=-1.0, acc=sub(nf, h, h + 1))
+                act(new(32), a[h], AF.Relu, bias=k1, scale=-1.0, acc=sub(nf, h, h + 1))
             act(off, nf, bias=kT, scale=-BIG)
-            dma("y", T.ho[t:t + 1, :], mine(H))
 
             def later_s():
                 for b in range(4):
                     act(A("DW", W * b + 256 + 64 * t, W * b + 320 + 64 * t), bank(2 + b, 64, 128), AF.Copy, scale=0.5)
-            bids(t + 1, [sub(V[0], 0, 256), sub(V[1], 0, 256)], [sub(off, 0, 1), sub(off, 1, 2)], later_s, lambda: cp(ind(LOC, so), pos))
+            bids(t + 1, [sub(V[0], 0, 256), sub(V[1], 0, 256)], [sub(off, 0, 1), sub(off, 1, 2)], later_s, lambda: t or cp(ind(H, so), GI))
             yn = act(new(64), bank(6, 64, 128), AF.Copy)
+            holders(t, "y")()
             cp(ind(P, so), NP)
             cp(ind(Y, so), yn)
             dma("y", T.pr[t:t + 1, :], mine(P))
         else:
             mm(6, Wc, Ws, *mov)
-            yn = act(new(64), bank(6, 64, 128), AF.Copy)
-            cp(ind(LOC, so), pos)
-            cp(ind(Y, so), yn)
-            lm = tt(new(32), sub(LOC, 32 * r, 32 * r + 32), CM, OP.mult)
-            dma("y", T.y[:], sub(Y, 0, 256))
-            l2 = new(2)
-            for c in range(2):
-                red(sub(l2, c, c + 1), sub(lm, 16 * c, 16 * c + 16))
-            oo = ts(new(2, "U"), l2, 0.125, OP.mult, wp, OP.subtract)
-            pick(A("Oc", 0, 32), A("Os", 0, 32), *Vw(0, 448), oo)
-            dma("y", T.oc[:], A("Oc", 0, 32))
             cp(ind(H, so), GI)
+            yn = act(new(64), bank(6, 64, 128), AF.Copy)
+            lm = tt(new(32), sub(H, 32 * r, 32 * r + 32), CM, OP.mult)
+            ho = holders(t, "s")
+            cp(ind(Y, so), yn)
+            dma("y", T.y[:], sub(Y, 0, 256))
+            l2 = scan(new(32), R16, lm, 0.0, OP.mult, OP.add)
+            ho()
+            oo = ts(new(2, "U"), sub(l2, 15, 32, 16), 2.0 ** -16, OP.mult, 0.25, OP.add)
+            pick(A("Oc", 0, 32), A("Os", 0, 32), *Vw(0, 448), oo)
+            pw = act(new(32), ind(PW, oo), AF.Copy)
+            dma("y", T.oc[:], A("Oc", 0, 32))
             for q in range(4):
                 dma("sy"[q % 2], T.osc[4 * q:4 * q + 4, :], A("Os", 0, 32, 1, (32 * q, 32 * q + 4)))
-            cp(ind(P, so), NP)
-            dma("s", T.ho[t:t + 1, :], mine(H))
-            dma("y", T.pr[t:t + 1, :], mine(P))
+            dma("s", T.pr[t:t + 1, :], one(pw))
 
     used = set()
     for o in ops:

from concourse.bass import DstId, RemoteDMATransfer
from concourse.mybir import dt, AluOpType as OP, AxisListType as AX, ActivationFunctionType as AF

PAIR = (0, 1, 3)
X4, U8 = "float8_e4m3fn_x4", "uint8"
W = 384
SCRATCH = {
    "F": ("sbuf", [128, 24576], "float32"), "C": ("sbuf", [128, 4096], "float32"), "N": ("sbuf", [128, 768], "bfloat16"),
    "U": ("sbuf", [128, 512], "uint16"), "L": ("sbuf", [128, 192], "float32"),
    "xb": ("sbuf", [128, 1024], "bfloat16"), "wb": ("sbuf", [128, 512], "bfloat16"), "Z": ("sbuf", [128, 520], "bfloat16"),
    "DX": ("sbuf", [128, 1024], "float32"), "DW": ("sbuf", [128, 4 * W], "float32"), "GX": ("sbuf", [128, 96], "float32"),
    "Xc": ("sbuf", [128, 256], X4), "Xs": ("sbuf", [128, 256], U8), "Pc": ("sbuf", [128, 256], X4), "Ps": ("sbuf", [128, 256], U8),
    "Wc": ("sbuf", [128, 128], X4), "Ws": ("sbuf", [128, 128], U8), "Ec": ("sbuf", [128, 512], X4), "Es": ("sbuf", [128, 512], U8),
    "Vc": ("sbuf", [128, 448], X4), "Vs": ("sbuf", [128, 448], U8), "Oc": ("sbuf", [128, 32], X4), "Os": ("sbuf", [128, 32], U8),
    "T0": ("sbuf", [128, 512], "bfloat16"), "T1": ("sbuf", [128, 576], "bfloat16"),
    "PS": ("psum", [128, 512 * 7], "float32"),
}
for _s in range(4):
    SCRATCH["Sc%d" % _s] = ("sbuf", [128, 256], X4)
    SCRATCH["Ss%d" % _s] = ("sbuf", [128, 256], U8)
SEMAPHORES = (["qv", "qs", "qt", "qg", "sent"] + ["d%d" % i for i in range(32)] + ["c%d" % i for i in range(4)]
              + ["p%d" % i for i in range(4)] + ["l%d" % i for i in range(3)])
BIG, TINY, PRED, MAG = 2.0 ** 96, 2.0 ** -90, 1.0 - 2.0 ** -24, 1.5 * 2.0 ** 23
STAGE = ((32, 0), (8, 256), (8, 320), (8, 384))


def A(n, a, b, s=1, p=(0, 128)):
    return (n, a, b, s, p[0], p[1])


def sub(v, a, b, s=1, p=None):
    return (v[0], v[1] + a, v[1] + b, s, v[4] if p is None else p[0], v[5] if p is None else p[1])


def rank_program(g, core, T, topo):
    r = T.rank_of(core)
    if r is None:
        return
    cores = list(T.cores)
    ops, log = [], {}
    Q = {"v": g.vector, "s": g.scalar, "t": g.tensor, "g": g, "y": g.sync}
    top = {"F": 0, "C": 0, "U": 0, "N": 0, "d": 0, "sent": 0}
    gv = g.vector

    def new(n, buf="F"):
        a = top[buf]
        top[buf] = a + (n + 15) // 16 * 16
        assert top[buf] <= SCRATCH[buf][1][1]
        return A(buf, a, a + n)

    def ap(v):
        if not isinstance(v, tuple):
            return v
        if v[0] == "ind":
            return ap(v[1]).indirect(ap(v[2]))
        return T[v[0]][v[4]:v[5], v[1]:v[2]] if v[3] == 1 else T[v[0]][v[4]:v[5], v[1]:v[2]:v[3]]

    def touch(v, i, q, write, deps):
        n, a, b, _, p0, p1 = v
        if n == "PS":
            a, b, p0, p1 = a // 512 * 512, (b + 511) // 512 * 512, 0, 128
        for (a2, b2, p2, p3, j, q2, w2) in log.setdefault(n, []):
            if j != i and a < b2 and a2 < b and p0 < p3 and p2 < p1 and (write or w2 or (n == "PS" and q2 != q)):
                deps.add(j)
        log[n].append((a, b, p0, p1, i, q, write))

    def op(q, fn, outs, ins, tok=None):
        i, deps = len(ops), set()
        for v, w in [(x, False) for x in ins] + [(x, True) for x in outs]:
            if isinstance(v, tuple):
                if v[0] == "ind":
                    touch(v[1], i, q, w, deps)
                    touch(v[2], i, q, False, deps)
                else:
                    touch(v, i, q, w, deps)
        ops.append({"q": q, "fn": fn, "deps": deps, "tok": tok})
        return outs[0] if outs else None

    def ts(o, i, s1, op0, s2=None, op1=None):
        if op1 is None:
            return op("v", lambda: gv.tensor_scalar(ap(o), ap(i), ap(s1), None, op0), [o], [i, s1])
        return op("v", lambda: gv.tensor_scalar(ap(o), ap(i), ap(s1), ap(s2), op0, op1), [o], [i, s1, s2])

    tt = lambda o, a, b, f: op("v", lambda: gv.tensor_tensor(ap(o), ap(a), ap(b), f), [o], [a, b])
    cp = lambda o, i: op("v", lambda: gv.tensor_copy(ap(o), ap(i)), [o], [i])
    red = lambda o, i, f=OP.add: op("v", lambda: gv.tensor_reduce(ap(o), ap(i), AX.X, f), [o], [i])
    scan = lambda o, d0, d1, init, f0, f1: op("v", lambda: gv.tensor_tensor_scan(ap(o), ap(d0), ap(d1), ap(init), f0, f1), [o], [d0, d1, init])
    tr = lambda o, i: op("v", lambda: gv.transpose(ap(o), ap(i)), [o], [i])
    ms = lambda o, c: op("v", lambda: gv.memset(ap(o), c), [o], [])
    quant = lambda c, s, i: op("v", lambda: gv.quantize_mx(ap(c), ap(s), ap(i)), [c, s], [i])

    def act(o, i, f=AF.Identity, bias=None, scale=None, acc=None):
        k = [(n, v) for n, v in (("bias", bias), ("scale", scale), ("accum_out", acc)) if v is not None]
        return op("s", lambda: g.scalar.activation(ap(o), ap(i), f, **{n: ap(v) for n, v in k}), [o, acc], [i, bias, scale])

    def ssum(o, i):
        act(new(i[2] - i[1]), i, acc=o)
        return o

    def mm(bank, lc, ls, rc, rs):
        o = A("PS", 512 * bank, 512 * bank + rc[2] - rc[1])
        op("t", lambda: g.tensor.matmul_mx(ap(o), ap(lc), ap(ls), ap(rc), ap(rs), True, True), [o], [lc, ls, rc, rs])

    def iota(o, pat, base=0, cm=0):
        if o is None:
            n = 1
            for s, c in pat:
                n *= c
            o = new(n, "C")
        return op("g", lambda: g.iota(ap(o), pat, base, cm, allow_small_or_imprecise_dtypes=True), [o], [])

    def raw(v):
        if isinstance(v, tuple) and SCRATCH[v[0]][2] == X4:
            return ap(v).bitcast(dt.uint8)
        return ap(v)

    def dma(q, o, i):
        sem = "d%d" % top["d"]
        top["d"] += 1
        op(q, lambda: Q[q].dma_start(raw(o), raw(i)).then_inc(T.sem[sem], 16), [o], [i], (sem, 16))

    def pick(oc, os, wc, ws, off):
        op("v", lambda: gv.tensor_copy(ap(oc).bitcast(dt.uint32), ap(wc).bitcast(dt.uint32).indirect(ap(off))), [oc], [wc, off])
        act(os, ("ind", ws, off), AF.Copy)

    sib = [q for q in range(8) if q != r and topo.chip(cores[q]) == topo.chip(core)][0]
    assert sib == r ^ 1
    u = r % 2
    off_chip = [q for q in range(8) if topo.chip(cores[q]) != topo.chip(core)]
    off_chip.sort(key=lambda q: (topo.die(cores[q]) == topo.die(core), topo.same_plane(topo.chip(core), topo.chip(cores[q])),
                                 topo.mates(topo.chip(core), topo.chip(cores[q]))))
    far = [q for q in off_chip if topo.die(cores[q]) == topo.die(core)]
    m_off = topo.mask(core, cores[off_chip[0]])
    m_on = topo.mask(core, cores[sib]) & ~m_off
    n_off, n_on = bin(m_off).count("1"), bin(m_on).count("1")

    def dst(q):
        a = topo.addr(cores[q])
        return DstId(rid=int(a[0]), pnc=int(a[1]))

    def call(parts):
        def fn():
            return g.remote_dma_fused([RemoteDMATransfer(dst_ids=[dst(q) for q in to], dma_engine_mask=m, remote_sem=T.sem[sem],
                                                         src=raw(s), dsts=[raw(d) for q in to]) for s, d, to, m, sem in parts], local_sem=T.sem.sent)
        top["sent"] += sum(bin(p[3]).count("1") for p in parts)
        op("g", fn, [], [p[0] for p in parts], ("none", 0))

    def arrive(views, sem, count):
        op("x", None, views, [], (sem, count))
        return sem

    def share_cols(st):
        n, base = STAGE[st]
        lo, hi, a, pl = base + n * r, base + n * (r + 1), 128 - n + n * u, base + n * (r - u)
        sc, vc, ss, vs = A("Sc%d" % st, a, a + n), A("Vc", lo, hi), A("Ss%d" % st, a, a + n), A("Vs", lo, hi)
        rest = lambda v, x0, x1: [A(v, x, y) for x, y in ((base, x0), (x1, base + 8 * n)) if x < y]
        if st not in PAIR:
            sem = arrive(rest("Vc", lo, hi) + rest("Vs", lo, hi), "c%d" % st, 2 * (n_off * len(off_chip) + n_on))
            for s, d in ((sc, vc), (ss, vs)):
                call([(s, d, off_chip, m_off, sem), (s, d, [sib], m_on, sem)])
                dma("y", d, s)
            return lambda: None
        sem = arrive(rest("Vc", lo, hi) + rest("Vs", pl, pl + 2 * n), "c%d" % st, n_off * (len(off_chip) + len(far)) + n_on)
        k = 4 * n if st else n
        wide = lambda who: A("Ss%d" % st, 128 - k + k * who, 128 + k * who)
        first = (wide(u), wide(u), [sib], m_on, arrive([wide(1 - u)], "p%d" % st, n_on))
        codes = [(sc, vc, off_chip, m_off, sem), (sc, vc, [sib], m_on, sem)]
        for parts in ([codes[0], first], codes[1:]) if st else ([first], codes):
            call(parts)
        dma("y", vc, sc)

        def hand_on():
            pair, vp = A("Ss%d" % st, 128 - n, 128 + n), A("Vs", pl, pl + 2 * n)
            call([(pair, vp, far, m_off, sem)])
            dma("y", vp, pair)
        return hand_on

    def share_list(t):
        b = 64 * t + 8 * (r - u)
        own, oth = A("L", b + 3 + 5 * u, b + 8 + 5 * u), A("L", b + 8 - 5 * u, b + 13 - 5 * u)
        rest = [A("L", x, y) for x, y in ((64 * t, b), (b + 16, 64 * t + 64)) if x < y]
        sem = arrive(rest + [oth], "l%d" % t, n_off * len(off_chip) + n_on)
        call([(own, own, off_chip, m_off, sem), (own, own, [sib], m_on, sem)])

    def quant_stage(st):
        a = 32 * max(st - 1, 0)
        quant(A("Sc%d" % st, 128 * u, 128 * u + 128), A("Ss%d" % st, 128 * u, 128 * u + 128), A("T%d" % min(st, 1), a, a + 512))

    dma("y", A("T0", 384 - 384 * u, 512 - 384 * u), T.it[:])
    dma("y", A("xb", 0, 1024), T.x[:])
    dma("y", A("wb", 0, 512), T.w[:])
    ID = iota(None, [[1, 128]], 0, -1)
    RW = new(192, "C")
    for i, pat in enumerate(([[1, 32]], [[0, 2], [1, 16]], [[0, 8], [1, 4]], [[0, 2], [1, 4], [0, 4]])):
        iota(sub(RW, 32 * i, 32 * i + 32), pat)
    xo = iota(None, [[32, 2], [64, 4], [16, 2]])
    ms(A("T0", 128 * u, 384 + 128 * u), 0.0)
    LM = ms(A("L", 0, 192), 0.0)
    ms(A("Z", 0, 516), 0.0)
    CB = [8192.0 * (256 + 64 * t + 8 * r) for t in range(3)]
    cst = new(16, "C")
    for i, c in enumerate([TINY, MAG, -MAG * 32768, MAG * 8192, -TINY, 1.0, 256.0] + [(-32767.5 - c) / 65536 for c in CB]):
        ms(sub(cst, i, i + 1), c)
    kT, kM, kM15, kM13, kN, k1, k256 = [sub(cst, i, i + 1) for i in range(7)]
    kO = [sub(cst, 7 + t, 8 + t) for t in range(3)]
    ts(A("Z", 3, 515, 4), ID, 0.0, OP.is_equal)
    op("g", None, [], [LM], ("none", 0))
    quant_stage(0)
    hand_on = share_cols(0)
    MP = new(224, "C")
    p2, mq = iota(None, [[32, 2]], 256 * r, 2), iota(None, [[1024, 4], [1, 8]], 0, -32)
    for i, pat, base in ((0, [[1000, 4], [1, 8]], -1000 * (r % 4)), (1, [[0, 2], [1, 8], [1000, 2]], 0), (4, [[0, 2], [1, 8], [-1000, 2]], 1000)):
        iota(sub(MP, 32 * i, 32 * i + 32), pat, base)
    hand_on()
    H = iota(new(320), [[8192, 320]], -1)
    for i, pat, base in ((4, [[0, 4], [1, 8]], 0), (5, [[0, 4], [16, 4], [5, 2]], 7)):
        iota(sub(RW, 32 * i, 32 * i + 32), pat, base)
    gb, trs = iota(None, [[16, 4], [0, 2]], 3), iota(None, [[16, 4], [-1000, 16]], 256)
    H2 = iota(new(320), [[2048, 320]])
    E = [(A("Ec", 128 * b, 128 * b + 128), A("Es", 128 * b, 128 * b + 128)) for b in range(4)]
    for b in range(4):
        quant(E[b][0], E[b][1], A("Z", 3 - b, 515 - b))
    Xc, Xs = A("Xc", 0, 256), A("Xs", 0, 256)
    RT = tr(new(128, "C"), sub(RW, 0, 128))
    quant(Xc, Xs, A("xb", 0, 1024))
    p32, p16, p4, q4 = [sub(RT, 32 * i, 32 * i + 1) for i in range(4)]
    XP = ts(new(16, "U"), xo, p16, OP.add)
    P = ms(new(320), 0.0)
    pick(A("Pc", 0, 256), A("Ps", 0, 256), Xc, Xs, XP)
    for b in range(4):
        mm(2 + b, E[b][0], E[b][1], Xc, Xs)
    for b in range(4):
        act(A("DX", 256 * b, 256 * b + 256), A("PS", 512 * (2 + b), 512 * (2 + b) + 256), AF.Copy, scale=0.5)
    Wc, Ws = A("Wc", 0, 128), A("Ws", 0, 128)
    quant(Wc, Ws, A("wb", 0, 512))
    CT = new(96, "C")
    ms(sub(CT, 32, 64), PRED)
    ms(sub(CT, 64, 96), 1.0)
    ms(A("T1", 0, 576), 0.0)
    t0 = ts(new(32, "C"), sub(RW, 0, 32), p32, OP.is_gt, 2.0 ** -24, OP.mult)
    q32 = ts(new(1, "C"), p32, 32.0, OP.mult)
    wq = ts(new(1, "C"), p4, float(W), OP.mult, 0.25, OP.add)
    xadd = ts(new(1, "C"), p4, 256.0, OP.mult, -256.0 * r, OP.add)
    TRI = ts(sub(CT, 0, 32), t0, PRED, OP.add)
    cp(sub(MP, 64, 96), sub(RW, 96, 128))
    ts(sub(MP, 96, 128), sub(RW, 96, 128), 4.0, OP.add)
    RS = ts(new(16, "C"), sub(RW, 0, 16), 8.0, OP.not_equal)
    gid2 = ts(new(2, "C"), p2, p32, OP.subtract)
    mapQ = ts(new(32, "C"), mq, q32, OP.add)
    cp(sub(MP, 160, 192), sub(MP, 0, 32))
    cp(sub(MP, 192, 224), sub(MP, 128, 160))
    gid = [ts(new(2, "C"), gid2, c, OP.add) for c in CB]
    ML = new(16, "C")
    for c in range(2):
        ts(sub(ML, 8 * c, 8 * c + 8), sub(MP, 128 + 8 * c, 136 + 8 * c), -4.0 * c, OP.add, q4, OP.is_equal)

    V = [new(320), new(320)]
    Y = new(320)
    PW = new(448)
    OG = new(4, "U")
    bank = lambda b, lo, hi: A("PS", 512 * b + lo, 512 * b + hi)
    Vw = lambda a, b: (A("Vc", a, b), A("Vs", a, b))
    Xp = lambda h: (A("Pc", 128 * h, 128 * h + 128), A("Ps", 128 * h, 128 * h + 128))
    ind = lambda w, o: ("ind", w, o)
    mine = lambda v: sub(v, 32 * r, 32 * r + 32, 1, (0, 1))
    one = lambda v: sub(v, 0, v[2] - v[1], 1, (0, 1))

    def bids(t, src, off, later_s, after_list):
        Fs, Ss, goal, gi, key = [new(256), new(256)], [new(256), new(256)], new(2), new(2), new(2)
        k = [sub(key, 0, 1), sub(key, 1, 2)]
        B = new(128)
        for h in range(2):
            scan(Fs[h], src[h], src[h] if t else sub(P, 0, 256), -BIG, OP.max, OP.max if t else OP.add)
            act(new(256), Fs[h], AF.Sign, bias=sub(Fs[h], 255, 256), scale=-1.0, acc=sub(goal, h, h + 1))
        for h in range(2):
            scan(sub(Ss[h], 0, 255), sub(src[h], 1, 256), sub(Fs[h], 0, 255), -BIG, OP.max, OP.min)
        act(k[0], act(new(1), sub(Ss[0], 254, 255), bias=sub(Fs[0], 255, 256), scale=-1.0), bias=off[0])
        act(sub(B, 0, 32), sub(CT, 64, 96), scale=k[0])
        act(sub(B, 96, 128), TRI, scale=k[0])
        ts(k[1], sub(Fs[1], 255, 256), sub(Ss[1], 254, 255), OP.subtract, off[1], OP.add)
        for h in range(2):
            act(sub(gi, h, h + 1), sub(goal, h, h + 1), bias=sub(gid[t], h, h + 1), scale=2048.0)
        later_s()
        ts(sub(B, 32, 96), sub(CT, 0, 64), k[1], OP.mult)
        B = tr(new(128), B)
        G, rk = new(128), [new(1), new(1)]
        for h in (1, 0):
            ts(sub(G, 64 * h, 64 * h + 64), sub(B, 64 - 64 * h, 128 - 64 * h), k[h], OP.is_ge)
        (ssum if t else red)(rk[1], sub(G, 64, 128))
        red(rk[0], sub(G, 0, 64))
        O = new(128)
        for h in range(2):
            for f, pay in enumerate((key, gi)):
                ts(sub(O, 64 * f + 32 * h, 64 * f + 32 * h + 32), mapQ, rk[h], OP.is_equal, sub(pay, h, h + 1), OP.mult)
        O = tr(new(128), O)
        P1, P2 = new(128), new(2)
        for f in range(2):
            scan(sub(P1, 64 * f, 64 * f + 64, 1, (0, 64)), sub(O, 64 * f, 64 * f + 64, 1, (0, 64)), sub(O, 64 * f, 64 * f + 64, 1, (64, 128)), 0.0, OP.add, OP.add)
        for a in (0, 32, 64, 96):
            tt(sub(P2, 0, 2, 1, (a, a + 32)), sub(P1, 63, 128, 64, (0, 32)), sub(P1, 63, 128, 64, (32, 64)), OP.add)
        ck, cg = sub(P2, 0, 1), sub(P2, 1, 2)
        B = ts(new(32), TRI, ck, OP.mult)
        y = ts(new(1), cg, -1023.5 - CB[t], OP.add, 2.0 ** -11, OP.mult)
        n = act(new(1), cg, bias=kO[t], scale=2.0 ** -16)
        n = act(new(1), n, bias=kM)
        n = act(new(1), n, bias=kM15, scale=32768.0)
        B = tr(new(32), B)
        gl = ts(new(1), y, MAG, OP.add, -MAG, OP.add)
        B = ts(new(32), B, ck, OP.is_ge)
        gs = ts(new(1), gl, 256.0, OP.mult, 8.0 * r, OP.add)
        r2 = red(new(1), B)
        cc = act(new(1), gs, bias=n)
        gd = ts(new(1), gl, -2048.0, OP.mult, cg, OP.add)
        O, Ot = new(288), new(288)
        oh = lambda a, b, m, pay: ts(sub(O, a, b), sub(MP, m, m + b - a), r2, OP.is_equal, pay, OP.mult)
        e = 288 if t + 1 in PAIR else 224
        oh(0, 64, 0, ck)
        oh(128, 192, 160, gl)
        oh(192, e, 32, gd)
        oh(64, 128, 128, cc)
        tr(sub(Ot, 0, e), sub(O, 0, e))
        m = 64 * t + 8 * (r - u) + 3 + 5 * u
        col = lambda f: A("L", m + f, m + f + 1)
        blk = lambda a, b: sub(Ot, 32 * a, 32 * b)
        ssum(col(1), blk(0, 1))
        red(col(4), blk(5, 7))
        red(col(0), blk(1, 3))
        ssum(col(3), blk(4, 5))
        red(col(2), blk(3, 4))
        share_list(t)
        if e < 288:
            oh(224, 288, 64, gd)
        og = ts(sub(OG, 2, 3) if t == 0 else sub(OG, 0, 1) if t == 1 else new(1, "U"), col(4), 255.0, OP.min)
        if e < 288:
            tr(sub(Ot, 224, 288), sub(O, 224, 288))
        after_list()
        x2 = new(2)
        for c in range(2):
            ssum(sub(x2, c, c + 1), blk(7 + c, 8 + c))
        lr = tt(new(16), ind(H, og), ML, OP.mult)
        ox = ts(new(2, "U"), x2, -CB[t], OP.add, xadd, OP.add)
        l2 = scan(new(16), RS, lr, 0.0, OP.mult, OP.add)
        gx = act(A("GX", 32 * t, 32 * t + 32), ind(A("DX", 0, 1024), ox), AF.Copy)
        ov = ts(new(2, "U"), sub(l2, 7, 16, 8), 2.0 ** -13, OP.mult, wq, OP.add)
        tt(A("T1", 32 * t + 480 - 480 * u, 32 * t + 512 - 480 * u), ind(A("DW", 0, 256 + 64 * t + 3 * W), ov), gx, OP.add)
        quant_stage(t + 1)
        share_cols(t + 1)()
        if t == 0:
            cp(sub(OG, 1, 2), og)
        return gi

    for h in range(2):
        mm(h, *Xp(h), *Vw(0, 256))
    for b in range(4):
        mm(2 + b, E[b][0], E[b][1], *Vw(0, 256))
    mm(6, Wc, Ws, *Vw(0, 256))

    def first_s():
        for b in range(4):
            act(A("DW", W * b, W * b + 256), bank(2 + b, 0, 256), AF.Copy, scale=0.5)
    gi = bids(0, [bank(0, 0, 256), bank(1, 0, 256)], [kT, kT], first_s, lambda: None)
    for h in range(2):
        act(sub(V[h], 0, 256), bank(h, 0, 256), AF.Copy)
    act(sub(Y, 0, 256), bank(6, 0, 256), AF.Copy)
    act(sub(PW, 0, 256), sub(P, 0, 256), AF.Copy)

    sl = tr(new(32, "C"), sub(MP, 128, 160))
    se = tr(new(32, "C"), sub(MP, 32, 64))
    RT = tr(new(64, "C"), sub(RW, 128, 192))
    par = ts(new(1, "C"), p32, p16, OP.subtract, 5.0 / 16, OP.mult)
    p8, gw = sub(RT, 0, 1), sub(RT, 32, 33)
    slot = ts(new(1, "C"), sub(sl, 0, 1), 8.0, OP.is_lt, sub(sl, 0, 1), OP.mult)
    slotw = ts(new(1, "C"), sub(se, 0, 1), 8.0, OP.is_lt, sub(se, 0, 1), OP.mult)
    GA = ts(new(8, "U"), gb, par, OP.add)
    GB = ts(new(8, "U"), gb, par, OP.add, 4.0, OP.add)
    GW = cp(new(1, "U"), gw)
    CM = ts(new(32, "C"), sub(RW, 32, 64), p16, OP.is_equal, 8.0, OP.mult)
    SR, GM = ts(new(32, "C"), sub(RW, 128, 160), 8192.0, OP.mult), []
    slotw = ts(new(1, "C"), slotw, 8192.0, OP.mult)
    ntr = new(2, "C")
    for b in range(2):
        ts(sub(ntr, b, b + 1), p32, -1.0, OP.mult, -256.0 - 32 * b, OP.add)
    kb1, kb2 = ts(new(1, "C"), p8, -32.0, OP.add, 1.0 / 128, OP.mult), ts(new(1, "C"), p8, 4096.0, OP.add, 1.0 / 16384, OP.mult)
    TRS = ts(new(64, "C"), trs, p16, OP.add)
    R16 = ts(new(32, "C"), sub(RW, 0, 32), 16.0, OP.not_equal)
    PR = new(32, "C")
    for c in range(2):
        ts(sub(PR, 16 * c, 16 * c + 16), sub(MP, 128, 144), 8192.0, OP.mult, CB[1 - c], OP.add)

    def sales(t):
        L = A("L", 64 * t, 64 * t + 64)
        t1 = tt(new(48), sub(L, 0, 48), sub(L, 16, 64), OP.add)
        IN = act(new(128), ind(L, GA), bias=slot)
        lo, hi = (0, 64), (64, 128)
        ow = new(2)
        for b, p in enumerate((lo, hi)):
            tt(sub(ow, 0, 2, 1, p), sub(t1, 4 + 32 * b, 6 + 32 * b, 1, p), sub(t1, 9 + 32 * b, 11 + 32 * b, 1, p), OP.add)
        R = tr(new(128), IN)
        K, G = sub(R, 0, 128, 2), sub(R, 1, 128, 2)
        b1 = act(new(1), sub(ow, 1, 2), bias=kb1, scale=1.0 / 128)
        b2 = act(new(1), sub(ow, 1, 2), bias=kb2, scale=1.0 / 16384)
        S = act(new(64), K, AF.Sign, bias=sub(ow, 0, 1), scale=-1.0)
        Q1 = act(new(64), G, AF.Square, bias=b1, scale=-1.0 / 128)
        Q2 = act(new(64), G, AF.Square, bias=b2, scale=-1.0 / 16384)
        GI = ts(new(128), ind(L, GB), slotw, OP.add)
        X1 = tt(new(64), S, Q1, OP.add)
        if t:
            po = ts(new(16, "U"), ind(L, GW), 255.0, OP.min)
        best = red(new(1), X1, OP.min)
        pw = sub(PW, 256 + 64 * t, 320 + 64 * t)
        NP = act(new(64) if t else pw, K, bias=kN)
        lose = act(new(1), best, bias=k256, scale=-4096.0)
        if t:
            PG = act(new(128), ind(P, sub(po, 0, 8)), AF.Copy)
        X2 = tt(new(64), Q2, S, OP.subtract)
        Wn = ts(new(64, "N"), X2, 0.06, OP.max, best, OP.is_lt)
        gl = tt(new(2), sub(t1, 6, 39, 32), sub(t1, 11, 44, 32), OP.add)
        Wn = tr(new(64, "N"), Wn)
        gm = tt(new(2), gl, ntr, OP.add)
        cn = [new(32), new(32)]
        for b, (own, oth) in enumerate(((lo, hi), (hi, lo))):
            for p in (lo, hi):
                scan(sub(cn[b], 0, 32, 1, p), sub(Wn, 32 * b, 32 * b + 32, 1, own), sub(Wn, 32 * b, 32 * b + 32, 1, oth), sub(lose, 0, 1, 1, own), OP.add, OP.add)
        B = new(64)
        for b in range(2):
            ts(sub(B, 32 * b, 32 * b + 32), CM, sub(cn[b], 31, 32), OP.is_gt, sub(gm, b, b + 1), OP.mult)
        B = tr(new(64), B)
        GI = tr(new(128), GI)
        B = scan(new(64), TRS, B, 0.0, OP.max, OP.add)
        if t:
            NP = tt(pw, sub(PG, 1, 128, 2), NP, OP.add)
        else:
            GM.append(tt(new(32), sub(GI, r // 4 * 64, r // 4 * 64 + 64, 2), SR, OP.subtract))
        return cp(new(4, "U"), sub(B, 15, 64, 16)), NP, sub(GI, 0, 128, 2)

    def holders(t, q):
        a = act(one(new(32)), mine(H), bias=one(kM), scale=2.0 ** -13)
        a = act(one(new(32)), a, bias=one(kM13), scale=-8192.0)
        return lambda: dma(q, T.ho[t:t + 1, :], tt(one(new(32)), a, mine(H), OP.add))

    for t in range(3):
        so, NP, GI = sales(t)
        mov = Vw(192 + 64 * t, 320 + 64 * t)
        if t < 2:
            for h in range(2):
                mm(h, *Xp(h), *mov)
            for b in range(4):
                mm(2 + b, E[b][0], E[b][1], *mov)
            mm(6, Wc, Ws, *mov)
            if t:
                cp(ind(H, so), GI)
                hg = tt(new(32), ind(sub(H, 0, 256), sub(OG, 0, 2)), PR, OP.subtract)
            else:
                hg = tt(new(32), ind(H2, sub(so, r // 4 * 2, r // 4 * 2 + 2)), GM[0], OP.add)
            vn = [tt(new(64), bank(h, 64, 128), NP, OP.subtract) for h in range(2)]
            for h in range(2):
                cp(ind(V[h], so), vn[h])
            nf, off = new(2), new(2)
            a = [act(new(32), hg, AF.Abs, bias=sub(gid2 if t else gi, h, h + 1), scale=-1.0) for h in range(2)]
            for h in range(2):
                act(new(32), a[h], AF.Relu, bias=k1, scale=-1.0, acc=sub(nf, h, h + 1))
            act(off, nf, bias=kT, scale=-BIG)

            def later_s():
                for b in range(4):
                    act(A("DW", W * b + 256 + 64 * t, W * b + 320 + 64 * t), bank(2 + b, 64, 128), AF.Copy, scale=0.5)
            bids(t + 1, [sub(V[0], 0, 256), sub(V[1], 0, 256)], [sub(off, 0, 1), sub(off, 1, 2)], later_s, lambda: t or cp(ind(H, so), GI))
            yn = act(new(64), bank(6, 64, 128), AF.Copy)
            holders(t, "y")()
            cp(ind(P, so), NP)
            cp(ind(Y, so), yn)
            dma("y", T.pr[t:t + 1, :], mine(P))
        else:
            mm(6, Wc, Ws, *mov)
            cp(ind(H, so), GI)
            yn = act(new(64), bank(6, 64, 128), AF.Copy)
            lm = tt(new(32), sub(H, 32 * r, 32 * r + 32), CM, OP.mult)
            ho = holders(t, "s")
            cp(ind(Y, so), yn)
            dma("y", T.y[:], sub(Y, 0, 256))
            l2 = scan(new(32), R16, lm, 0.0, OP.mult, OP.add)
            ho()
            oo = ts(new(2, "U"), sub(l2, 15, 32, 16), 2.0 ** -16, OP.mult, 0.25, OP.add)
            pick(A("Oc", 0, 32), A("Os", 0, 32), *Vw(0, 448), oo)
            pw = act(new(32), ind(PW, oo), AF.Copy)
            dma("y", T.oc[:], A("Oc", 0, 32))
            for q in range(4):
                dma("sy"[q % 2], T.osc[4 * q:4 * q + 4, :], A("Os", 0, 32, 1, (32 * q, 32 * q + 4)))
            dma("s", T.pr[t:t + 1, :], one(pw))

    used = set()
    for o in ops:
        last = {}
        for j in o["deps"]:
            if ops[j]["tok"] is None:
                last[ops[j]["q"]] = max(last.get(ops[j]["q"], -1), j)
        used.update(last.values())
        o["deps"] = [j for j in o["deps"] if ops[j]["tok"] is not None] + list(last.values())
    count, seen, total = {"v": 0, "s": 0, "t": 0, "g": 0}, {}, {"sent": top["sent"]}
    for i, o in enumerate(ops):
        q = o["q"]
        if q == "x":
            total[o["tok"][0]] = o["tok"][1]
            continue
        need = {}
        for j in o["deps"]:
            s, c = ops[j]["tok"]
            need[s] = max(need.get(s, 0), c)
        for s, c in sorted(need.items()):
            if c > seen.get((q, s), 0):
                Q[q].wait_ge(T.sem[s], c)
                seen[(q, s)] = c
        if o["fn"] is None:
            continue
        ins = o["fn"]()
        if o["tok"] is None:
            if i in used:
                count[q] += 1
                ins.then_inc(T.sem["q" + q], 1)
                o["tok"] = ("q" + q, count[q])
                total["q" + q] = count[q]
        elif o["tok"][1]:
            total[o["tok"][0]] = o["tok"][1]
    for s, c in total.items():
        if c > max([0] + [v for (q, s2), v in seen.items() if s2 == s]):
            g.wait_ge(T.sem[s], c)
